import numpy as np
import ml_dtypes


def mxq(x, axis, fmt="e4m3"):
    dtype, down = {"e4m3": (ml_dtypes.float8_e4m3fn, 7), "e5m2": (ml_dtypes.float8_e5m2, 14)}[fmt]
    v = np.moveaxis(np.asarray(x, np.float32).astype(ml_dtypes.bfloat16).astype(np.float64), axis, -1)
    blocks = v.reshape(v.shape[:-1] + (-1, 32))
    amax = np.abs(blocks).max(-1, keepdims=True)
    byte = np.maximum(np.where(amax > 0, np.frexp(amax)[1] - 1 + 127, 0) - down, 1)
    scale = np.exp2(byte - 127.0)
    codes = (blocks / scale).astype(np.float32).astype(dtype).astype(np.float64)
    return np.moveaxis((codes * scale).reshape(v.shape), -1, axis)


WIDE = False


def mx_kscale(k):
    if not WIDE:
        return np.ones(k)
    levels = np.array([10, -10, 5, -5, 0])
    if k % 512:
        return np.exp2(np.random.permutation(np.resize(levels, k // 32))).repeat(32)
    a = np.empty((k // 512, 16))
    for p in range(k // 512):
        a[p, :8] = np.random.permutation(np.resize(levels, 8))
        for g in range(8):
            far = levels[np.abs(levels - a[p, g]) >= 10]
            a[p, g + 8] = far[np.random.randint(len(far))]
    return np.exp2(a.ravel()).repeat(32)


def f64(x):
    return np.asarray(x).astype(np.float64)


def striped(idx):
    return np.tile(idx.reshape(-1, 16).T, (8, 1)).astype(np.uint16)


def unstriped(offs):
    return offs[:16].T.reshape(-1).astype(np.int64)


def striped8(idx):
    return np.concatenate([x.reshape(-1, 16).T for x in idx]).astype(np.uint16)


def runs(offs, k):
    lists = np.stack([offs[16 * r : 16 * r + 16].T.reshape(-1) for r in range(8)]).astype(np.int64)
    return lists[np.arange(k) % 512 // 64]


def pack_weight(w):
    k, n = w.shape
    w = f64(np.asarray(w, np.float32).astype(ml_dtypes.bfloat16)).reshape(k // 32, 32, n)
    amax = np.abs(w).max(1)
    byte = np.clip(np.where(amax > 0, np.frexp(amax)[1] - 1 + 127 - 7, 1), 1, 254)
    scaled = (w * np.exp2(127.0 - byte)[:, None, :]).reshape(k, n).astype(np.float32)
    words = np.ascontiguousarray(scaled.reshape(k // 512, 128, 4, n).transpose(0, 1, 3, 2)).astype(ml_dtypes.float8_e4m3fn).view(np.uint8)
    return words, np.ascontiguousarray(byte.astype(np.uint8).reshape(k // 512, 16, n))


def unpack_weight(words, scales):
    g, p, n, _ = words.shape
    vals = np.ascontiguousarray(words).view(ml_dtypes.float8_e4m3fn).astype(np.float64) * np.repeat(np.exp2(scales.astype(np.float64) - 127.0), 8, axis=1)[..., None]
    return vals.transpose(0, 1, 3, 2).reshape(g * 512, n)


K, T, S, V, H = 512, 2048, 512, 256, 512


def setup_inputs():
    n = np.random.standard_normal
    s = mx_kscale(K)[:, None]
    u = mx_kscale(S)
    packed_xT = pack_weight(n((K, T)) * s)
    return {
        "x_words": packed_xT[0],
        "x_scales": packed_xT[1],
        "wa": (n((K, H)) / np.sqrt(K) / s).astype(np.float32),
        "wb": (n((K, H)) / np.sqrt(K) / s).astype(np.float32),
        "gt": (np.random.uniform(0.5, 1.5, (S, 1)) * u[:, None]).astype(np.float32),
        "gi": (np.random.uniform(0.5, 1.5, (S, 1)) / u[:, None]).astype(np.float32),
        "offs": striped(np.random.permutation(T)[:S]),
        "fa": striped8(np.stack([np.random.permutation(H)[:V] for _ in range(8)])),
    }


def reference(x_words, x_scales, wa, wb, gt, gi, offs, fa):
    xq = unpack_weight(x_words, x_scales)[:, unstriped(offs)]
    b = xq.T @ mxq(f64(wb), 0, "e4m3")
    z = f64(gt) * b
    a = xq.T @ mxq(f64(wa), 0, "e4m3")
    z2 = f64(gi) * (a[np.arange(S)[:, None], runs(fa, S)])
    return 0.0625 * ((mxq(z, 0, "e4m3").T @ mxq(z2, 0, "e4m3")))

@@ -1,0 +1,145 @@
+from contextlib import ExitStack
+
+import concourse.mybir as mybir
+
+K, T, S, V, H = 512, 2048, 512, 256, 512
+FLOPS = 2 * K * S * H * 2 + 2 * S * H * V
+
+F32 = mybir.dt.float32
+BF16 = mybir.dt.bfloat16
+I32 = mybir.dt.int32
+U32 = mybir.dt.uint32
+U16 = mybir.dt.uint16
+U8 = mybir.dt.uint8
+FP8X4 = mybir.dt.float8_e4m3fn_x4
+COPY = mybir.ActivationFunctionType.Copy
+MULT = mybir.AluOpType.mult
+
+P = 128
+PACK = 4
+HALF = 256
+CHUNK = 128
+
+
+def weave(copy, dst, src, c0, c1):
+    copy(dst[:, c0:c1, :].rearrange("p (c i) t -> p c t i", i=4), src[:, :, c0:c1].rearrange("p t (c i) -> p c t i", i=4))
+
+
+def quantise(nc, pool, woven, width, name):
+    codes = pool.tile([P, width], U32, name=name + "_codes", align_bytes=64)
+    scales = pool.tile([P, width], U8, name=name + "_scales", align_bytes=64)
+    nc.vector.quantize_mx(out=codes[:].bitcast(FP8X4), scales=scales[:], in_=woven[:].rearrange("p c t -> p (c t)"))
+    return codes, scales
+
+
+def tile_picked_gramsel_none_p_kernel(tc, x_words, x_scales, wa, wb, gt, gi, offs, fa, out):
+    nc = tc.nc
+    with ExitStack() as ctx:
+        keep = ctx.enter_context(tc.tile_pool(name="keep", bufs=1))
+        psum = ctx.enter_context(tc.psum_pool(name="psum", bufs=1))
+
+        offs_sb = keep.tile([P, S // 16], U16, name="offs_sb")
+        fa_sb = keep.tile([P, V // 16], U16, name="fa_sb")
+        xw = keep.tile([P, T], U32, name="xw", align_bytes=64)
+        xs = keep.tile([P, T], U8, name="xs", align_bytes=64)
+        gt_sb = keep.tile([P, PACK], F32, name="gt_sb")
+        gi_sb = keep.tile([P, PACK], F32, name="gi_sb")
+
+        nc.vector.memset(xs[:].bitcast(I32), 0)
+        nc.sync.dma_start(offs_sb[:], offs)
+        for q in range(4):
+            nc.scalar.dma_start(xs[32 * q : 32 * q + 4, :].bitcast(I32), x_scales[0, 4 * q : 4 * q + 4, :].bitcast(I32))
+        nc.sync.dma_start(xw[:].bitcast(I32), x_words[0].rearrange("p n t -> p (n t)").bitcast(I32))
+
+        def load_half(w, h, name):
+            raw = keep.tile([P, PACK, HALF], F32, name=name)
+            nc.sync.dma_start(raw[:], w[:, h * HALF : (h + 1) * HALF].rearrange("(p t) c -> p t c", t=PACK))
+            return raw
+
+        wa_raw = [load_half(wa, h, "wa_raw%d" % h) for h in range(2)]
+        nc.sync.dma_start(gi_sb[:], gi.rearrange("(p t) o -> p (t o)", t=PACK))
+        nc.sync.dma_start(fa_sb[:], fa)
+        nc.sync.dma_start(gt_sb[:], gt.rearrange("(p t) o -> p (t o)", t=PACK))
+        wb_raw = [load_half(wb, h, "wb_raw%d" % h) for h in range(2)]
+
+        sg = keep.tile([P, S], U8, name="sg", align_bytes=64)
+        nc.vector.tensor_copy(sg[:], xs[:].indirect(offs_sb[:]))
+        xq_scales = keep.tile([P, S], U8, name="xq_scales", align_bytes=64)
+        nc.vector.tensor_copy(xq_scales[:].rearrange("p (t m) -> p t m", t=PACK), sg[:].rearrange("p (m t) -> p t m", t=PACK))
+        xq_codes = keep.tile([P, S], U32, name="xq_codes", align_bytes=64)
+        nc.vector.tensor_copy(xq_codes[:].rearrange("p (t m) -> p m t", t=PACK), xw[:].indirect(offs_sb[:]))
+
+        def project(dst, t, codes, scales, c0, c1):
+            nc.tensor.matmul_mx(
+                out=dst,
+                lhsT=xq_codes[:, t * P : (t + 1) * P].bitcast(FP8X4),
+                lhsT_scale=xq_scales[:, t * P : (t + 1) * P],
+                rhs=codes[:, c0:c1].bitcast(FP8X4),
+                rhs_scale=scales[:, c0:c1],
+                start=True,
+                stop=True,
+            )
+
+        a_rows = [keep.tile([P, H], F32, name="a_rows%d" % t) for t in range(PACK)]
+        for h in range(2):
+            woven = keep.tile([P, HALF, PACK], BF16, name="wa_woven%d" % h, align_bytes=64)
+            if h == 0:
+                weave(nc.vector.tensor_copy, woven, wa_raw[h], 0, HALF)
+            else:
+                weave(nc.scalar.copy, woven, wa_raw[h], 160, HALF)
+                weave(nc.vector.tensor_copy, woven, wa_raw[h], 0, 160)
+            codes, scales = quantise(nc, keep, woven, HALF, "wa%d" % h)
+            for pair in range(2):
+                bank = psum.tile([P, 2, HALF], F32, name="a_bank", tag="bank%d" % (2 * h + pair))
+                for u in range(2):
+                    project(bank[:, u, :], 2 * pair + u, codes, scales, 0, HALF)
+                for u in range(2):
+                    t = 2 * pair + u
+                    nc.scalar.activation(a_rows[t][:, h * HALF : (h + 1) * HALF], bank[:, u, :], COPY, scale=gi_sb[:, t : t + 1])
+
+        z2_planes = keep.tile([P, PACK, V], BF16, name="z2_planes", align_bytes=64)
+        for t in range(PACK):
+            nc.vector.tensor_copy(z2_planes[:, t, :], a_rows[t][:].indirect(fa_sb[:]))
+
+        wb_q = []
+        for h in range(2):
+            woven = keep.tile([P, HALF, PACK], BF16, name="wb_woven%d" % h, align_bytes=64)
+            weave(nc.scalar.copy, woven, wb_raw[h], 0, HALF)
+            if h == 0:
+                z2_woven = keep.tile([P, V, PACK], BF16, name="z2_woven", align_bytes=64)
+                weave(nc.vector.tensor_copy, z2_woven, z2_planes, 0, V)
+            wb_q.append(quantise(nc, keep, woven, HALF, "wb%d" % h))
+            if h == 0:
+                z2_codes, z2_scales = quantise(nc, keep, z2_woven, V, "z2")
+
+        gt_spread = gt_sb[:].rearrange("p (o t) -> p o t", o=1).to_broadcast([P, CHUNK, PACK])
+        z_woven = []
+        for c in range(H // CHUNK):
+            codes, scales = wb_q[c // 2]
+            bank = psum.tile([P, PACK, CHUNK], F32, name="b_bank", tag="bank%d" % (4 + c))
+            for t in range(PACK):
+                project(bank[:, t, :], t, codes, scales, (c % 2) * CHUNK, (c % 2 + 1) * CHUNK)
+            z_woven.append((bank, keep.tile([P, CHUNK, PACK], BF16, name="z_woven%d" % c, align_bytes=64)))
+
+        def finish(c):
+            codes, scales = quantise(nc, keep, z_woven[c][1], CHUNK, "zchunk%d" % c)
+            bank = psum.tile([P, V], F32, name="out_bank", tag="bank%d" % c)
+            nc.tensor.matmul_mx(
+                out=bank[:],
+                lhsT=codes[:].bitcast(FP8X4),
+                lhsT_scale=scales[:],
+                rhs=z2_codes[:].bitcast(FP8X4),
+                rhs_scale=z2_scales[:],
+                start=True,
+                stop=True,
+            )
+            result = keep.tile([P, V], F32, name="result%d" % c)
+            nc.scalar.activation(result[:], bank[:], COPY, scale=0.0625)
+            nc.sync.dma_start(out[c * CHUNK : (c + 1) * CHUNK, :], result[:])
+
+        for c in range(H // CHUNK):
+            bank, woven = z_woven[c]
+            nc.vector.tensor_tensor(woven[:], bank[:].rearrange("p t n -> p n t"), gt_spread, MULT)
+            if c > 0:
+                finish(c - 1)
+        finish(H // CHUNK - 1)

@@ -14,6 +14,7 @@ U8 = mybir.dt.uint8
 FP8X4 = mybir.dt.float8_e4m3fn_x4
 COPY = mybir.ActivationFunctionType.Copy
 MULT = mybir.AluOpType.mult
+ADD = mybir.AluOpType.add
 
 P = 128
 PACK = 4
@@ -35,111 +36,125 @@ def quantise(nc, pool, woven, width, name):
 def tile_picked_gramsel_none_p_kernel(tc, x_words, x_scales, wa, wb, gt, gi, offs, fa, out):
     nc = tc.nc
     with ExitStack() as ctx:
+        lists = ctx.enter_context(tc.tile_pool(name="lists", bufs=1))
         keep = ctx.enter_context(tc.tile_pool(name="keep", bufs=1))
         psum = ctx.enter_context(tc.psum_pool(name="psum", bufs=1))
 
-        offs_sb = keep.tile([P, S // 16], U16, name="offs_sb")
-        fa_sb = keep.tile([P, V // 16], U16, name="fa_sb")
+        offs_sb = lists.tile([P, S // 16], U16, name="offs_sb")
+        fa_sb = lists.tile([P, V // 16], U16, name="fa_sb")
         xw = keep.tile([P, T], U32, name="xw", align_bytes=64)
         xs = keep.tile([P, T], U8, name="xs", align_bytes=64)
         gt_sb = keep.tile([P, PACK], F32, name="gt_sb")
-        gi_sb = keep.tile([P, PACK], F32, name="gi_sb")
-
-        nc.vector.memset(xs[:].bitcast(I32), 0)
-        nc.sync.dma_start(offs_sb[:], offs)
-        for q in range(4):
-            nc.scalar.dma_start(xs[32 * q : 32 * q + 4, :].bitcast(I32), x_scales[0, 4 * q : 4 * q + 4, :].bitcast(I32))
-        nc.sync.dma_start(xw[:].bitcast(I32), x_words[0].rearrange("p n t -> p (n t)").bitcast(I32))
+        gi_sb = keep.tile([P, PACK], F32, name="gi_sb", tag="after_a", align_bytes=64)
 
         def load_half(w, h, name):
-            raw = keep.tile([P, PACK, HALF], F32, name=name)
+            raw = keep.tile([P, PACK, HALF], F32, name=name, tag=name, align_bytes=64)
             nc.sync.dma_start(raw[:], w[:, h * HALF : (h + 1) * HALF].rearrange("(p t) c -> p t c", t=PACK))
             return raw
 
-        wa_raw = [load_half(wa, h, "wa_raw%d" % h) for h in range(2)]
-        nc.sync.dma_start(gi_sb[:], gi.rearrange("(p t) o -> p (t o)", t=PACK))
+        xs_rows = keep.tile([P, T], U8, name="xs_rows", align_bytes=64)
+        for q in range(4):
+            queue = nc.sync if q % 2 == 0 else nc.scalar
+            queue.dma_start(xs_rows[32 * q : 32 * q + 4, :].bitcast(I32), x_scales[0, 4 * q : 4 * q + 4, :].bitcast(I32))
+        nc.scalar.dma_start(gi_sb[:], gi.rearrange("(p t) o -> p (t o)", t=PACK))
+        nc.sync.dma_start(offs_sb[:], offs)
+        nc.sync.dma_start(xw[:].bitcast(I32), x_words[0].rearrange("p n t -> p (n t)").bitcast(I32))
+        wa_raw0 = load_half(wa, 0, "wa_raw0")
+        wa_raw1 = load_half(wa, 1, "wa_raw1")
         nc.sync.dma_start(fa_sb[:], fa)
         nc.sync.dma_start(gt_sb[:], gt.rearrange("(p t) o -> p (t o)", t=PACK))
         wb_raw = [load_half(wb, h, "wb_raw%d" % h) for h in range(2)]
 
+        nc.vector.memset(xs[:].bitcast(I32), 0)
+        for q in range(4):
+            nc.vector.tensor_copy(xs[32 * q : 32 * q + 4, :].bitcast(I32), xs_rows[32 * q : 32 * q + 4, :].bitcast(I32))
         sg = keep.tile([P, S], U8, name="sg", align_bytes=64)
         nc.vector.tensor_copy(sg[:], xs[:].indirect(offs_sb[:]))
-        xq_scales = keep.tile([P, S], U8, name="xq_scales", align_bytes=64)
-        nc.vector.tensor_copy(xq_scales[:].rearrange("p (t m) -> p t m", t=PACK), sg[:].rearrange("p (m t) -> p t m", t=PACK))
+
+        def woven_tile(name, tag):
+            return keep.tile([P, HALF, PACK], BF16, name=name, tag=tag, align_bytes=64)
+
         xq_codes = keep.tile([P, S], U32, name="xq_codes", align_bytes=64)
         nc.vector.tensor_copy(xq_codes[:].rearrange("p (t m) -> p m t", t=PACK), xw[:].indirect(offs_sb[:]))
+        xq_scales = keep.tile([P, S], U8, name="xq_scales", align_bytes=64)
+        nc.vector.tensor_copy(xq_scales[:].rearrange("p (t m) -> p t m", t=PACK), sg[:].rearrange("p (m t) -> p t m", t=PACK))
+        wa_woven0 = woven_tile("wa_woven0", "wa_woven0")
+        weave(nc.scalar.copy, wa_woven0, wa_raw0, 64, HALF)
+        weave(nc.vector.tensor_copy, wa_woven0, wa_raw0, 0, 64)
+        wa_q0 = quantise(nc, keep, wa_woven0, HALF, "wa0")
 
-        def project(dst, t, codes, scales, c0, c1):
+        def project(t, quantised, bank):
+            codes, scales = quantised
+            sums = psum.tile([P, HALF], F32, name="sums", tag="bank%d" % bank)
             nc.tensor.matmul_mx(
-                out=dst,
+                out=sums[:],
                 lhsT=xq_codes[:, t * P : (t + 1) * P].bitcast(FP8X4),
                 lhsT_scale=xq_scales[:, t * P : (t + 1) * P],
-                rhs=codes[:, c0:c1].bitcast(FP8X4),
-                rhs_scale=scales[:, c0:c1],
+                rhs=codes[:].bitcast(FP8X4),
+                rhs_scale=scales[:],
                 start=True,
                 stop=True,
             )
+            return sums
 
+        wa_woven1 = woven_tile("wa_woven1", "after_wa")
+        weave(nc.scalar.copy, wa_woven1, wa_raw1, 144, HALF)
+        weave(nc.vector.tensor_copy, wa_woven1, wa_raw1, 0, 144)
+        wa_q1 = quantise(nc, keep, wa_woven1, HALF, "wa1")
         a_rows = [keep.tile([P, H], F32, name="a_rows%d" % t) for t in range(PACK)]
-        for h in range(2):
-            woven = keep.tile([P, HALF, PACK], BF16, name="wa_woven%d" % h, align_bytes=64)
-            if h == 0:
-                weave(nc.vector.tensor_copy, woven, wa_raw[h], 0, HALF)
-            else:
-                weave(nc.scalar.copy, woven, wa_raw[h], 160, HALF)
-                weave(nc.vector.tensor_copy, woven, wa_raw[h], 0, 160)
-            codes, scales = quantise(nc, keep, woven, HALF, "wa%d" % h)
-            for pair in range(2):
-                bank = psum.tile([P, 2, HALF], F32, name="a_bank", tag="bank%d" % (2 * h + pair))
-                for u in range(2):
-                    project(bank[:, u, :], 2 * pair + u, codes, scales, 0, HALF)
-                for u in range(2):
-                    t = 2 * pair + u
-                    nc.scalar.activation(a_rows[t][:, h * HALF : (h + 1) * HALF], bank[:, u, :], COPY, scale=gi_sb[:, t : t + 1])
+        for h, t in ((0, 0), (0, 1), (1, 0), (0, 2), (1, 1), (0, 3), (1, 2), (1, 3)):
+            sums = project(t, wa_q1 if h else wa_q0, PACK * h + t)
+            nc.scalar.activation(a_rows[t][:, h * HALF : (h + 1) * HALF], sums[:], COPY, scale=gi_sb[:, t : t + 1])
 
         z2_planes = keep.tile([P, PACK, V], BF16, name="z2_planes", align_bytes=64)
-        for t in range(PACK):
+
+        def look_up(t):
             nc.vector.tensor_copy(z2_planes[:, t, :], a_rows[t][:].indirect(fa_sb[:]))
 
-        wb_q = []
-        for h in range(2):
-            woven = keep.tile([P, HALF, PACK], BF16, name="wb_woven%d" % h, align_bytes=64)
-            weave(nc.scalar.copy, woven, wb_raw[h], 0, HALF)
-            if h == 0:
-                z2_woven = keep.tile([P, V, PACK], BF16, name="z2_woven", align_bytes=64)
-                weave(nc.vector.tensor_copy, z2_woven, z2_planes, 0, V)
-            wb_q.append(quantise(nc, keep, woven, HALF, "wb%d" % h))
-            if h == 0:
-                z2_codes, z2_scales = quantise(nc, keep, z2_woven, V, "z2")
-
-        gt_spread = gt_sb[:].rearrange("p (o t) -> p o t", o=1).to_broadcast([P, CHUNK, PACK])
-        z_woven = []
-        for c in range(H // CHUNK):
-            codes, scales = wb_q[c // 2]
-            bank = psum.tile([P, PACK, CHUNK], F32, name="b_bank", tag="bank%d" % (4 + c))
+        def z_half(quantised, first_bank, name, tag):
+            planes = keep.tile([P, PACK, HALF], BF16, name=name, tag=tag, align_bytes=64)
             for t in range(PACK):
-                project(bank[:, t, :], t, codes, scales, (c % 2) * CHUNK, (c % 2 + 1) * CHUNK)
-            z_woven.append((bank, keep.tile([P, CHUNK, PACK], BF16, name="z_woven%d" % c, align_bytes=64)))
+                sums = project(t, quantised, first_bank + t)
+                nc.scalar.activation(planes[:, t, :], sums[:], COPY, scale=gt_sb[:, t : t + 1])
+            return planes
 
-        def finish(c):
-            codes, scales = quantise(nc, keep, z_woven[c][1], CHUNK, "zchunk%d" % c)
+        wb_woven0 = woven_tile("wb_woven0", "after_wa")
+        weave(nc.vector.tensor_copy, wb_woven0, wb_raw[0], 0, HALF)
+        wb_q0 = quantise(nc, keep, wb_woven0, HALF, "wb0")
+        wb_woven1 = woven_tile("wb_woven1", "wb_raw0")
+        weave(nc.vector.tensor_copy, wb_woven1, wb_raw[1], 0, HALF)
+        look_up(0)
+        wb_q1 = quantise(nc, keep, wb_woven1, HALF, "wb1")
+        for t in range(1, PACK):
+            look_up(t)
+        z_planes0 = z_half(wb_q0, 0, "z_planes0", "after_a")
+        z_planes1 = z_half(wb_q1, PACK, "z_planes1", "z_planes1")
+        z_woven0 = woven_tile("z_woven0", "z_woven0")
+        weave(nc.vector.tensor_copy, z_woven0, z_planes0, 0, HALF)
+        z2_woven = woven_tile("z2_woven", "after_a")
+        weave(nc.vector.tensor_copy, z2_woven, z2_planes, 0, V)
+        z_woven1 = woven_tile("z_woven1", "z_woven1")
+        weave(nc.scalar.copy, z_woven1, z_planes1, 0, HALF)
+        z_q0 = quantise(nc, keep, z_woven0, HALF, "zhalf0")
+        z2_codes, z2_scales = quantise(nc, keep, z2_woven, V, "z2")
+        z_q1 = quantise(nc, keep, z_woven1, HALF, "zhalf1")
+
+        for c in range(H // CHUNK):
+            codes, scales = z_q1 if c // 2 else z_q0
+            cols = slice((c % 2) * CHUNK, (c % 2 + 1) * CHUNK)
             bank = psum.tile([P, V], F32, name="out_bank", tag="bank%d" % c)
             nc.tensor.matmul_mx(
                 out=bank[:],
-                lhsT=codes[:].bitcast(FP8X4),
-                lhsT_scale=scales[:],
+                lhsT=codes[:, cols].bitcast(FP8X4),
+                lhsT_scale=scales[:, cols],
                 rhs=z2_codes[:].bitcast(FP8X4),
                 rhs_scale=z2_scales[:],
                 start=True,
                 stop=True,
             )
             result = keep.tile([P, V], F32, name="result%d" % c)
-            nc.scalar.activation(result[:], bank[:], COPY, scale=0.0625)
+            if c % 2:
+                nc.vector.tensor_scalar(result[:], bank[:], 0.0625, None, MULT)
+            else:
+                nc.scalar.activation(result[:], bank[:], COPY, scale=0.0625)
             nc.sync.dma_start(out[c * CHUNK : (c + 1) * CHUNK, :], result[:])
-
-        for c in range(H // CHUNK):
-            bank, woven = z_woven[c]
-            nc.vector.tensor_tensor(woven[:], bank[:].rearrange("p t n -> p n t"), gt_spread, MULT)
-            if c > 0:
-                finish(c - 1)
-        finish(H // CHUNK - 1)

@@ -56,14 +56,15 @@ def tile_picked_gramsel_none_p_kernel(tc, x_words, x_scales, wa, wb, gt, gi, off
         for q in range(4):
             queue = nc.sync if q % 2 == 0 else nc.scalar
             queue.dma_start(xs_rows[32 * q : 32 * q + 4, :].bitcast(I32), x_scales[0, 4 * q : 4 * q + 4, :].bitcast(I32))
-        nc.scalar.dma_start(gi_sb[:], gi.rearrange("(p t) o -> p (t o)", t=PACK))
         nc.sync.dma_start(offs_sb[:], offs)
         nc.sync.dma_start(xw[:].bitcast(I32), x_words[0].rearrange("p n t -> p (n t)").bitcast(I32))
         wa_raw0 = load_half(wa, 0, "wa_raw0")
         wa_raw1 = load_half(wa, 1, "wa_raw1")
+        nc.sync.dma_start(gi_sb[:], gi.rearrange("(p t) o -> p (t o)", t=PACK))
+        wb_raw = [load_half(wb, 0, "wb_raw0")]
         nc.sync.dma_start(fa_sb[:], fa)
+        wb_raw.append(load_half(wb, 1, "wb_raw1"))
         nc.sync.dma_start(gt_sb[:], gt.rearrange("(p t) o -> p (t o)", t=PACK))
-        wb_raw = [load_half(wb, h, "wb_raw%d" % h) for h in range(2)]
 
         nc.vector.memset(xs[:].bitcast(I32), 0)
         for q in range(4):
@@ -79,8 +80,7 @@ def tile_picked_gramsel_none_p_kernel(tc, x_words, x_scales, wa, wb, gt, gi, off
         xq_scales = keep.tile([P, S], U8, name="xq_scales", align_bytes=64)
         nc.vector.tensor_copy(xq_scales[:].rearrange("p (t m) -> p t m", t=PACK), sg[:].rearrange("p (m t) -> p t m", t=PACK))
         wa_woven0 = woven_tile("wa_woven0", "wa_woven0")
-        weave(nc.scalar.copy, wa_woven0, wa_raw0, 64, HALF)
-        weave(nc.vector.tensor_copy, wa_woven0, wa_raw0, 0, 64)
+        weave(nc.scalar.copy, wa_woven0, wa_raw0, 0, HALF)
         wa_q0 = quantise(nc, keep, wa_woven0, HALF, "wa0")
 
         def project(t, quantised, bank):
@@ -118,7 +118,7 @@ def tile_picked_gramsel_none_p_kernel(tc, x_words, x_scales, wa, wb, gt, gi, off
                 nc.scalar.activation(planes[:, t, :], sums[:], COPY, scale=gt_sb[:, t : t + 1])
             return planes
 
-        wb_woven0 = woven_tile("wb_woven0", "after_wa")
+        wb_woven0 = woven_tile("wb_woven0", "wa_raw1")
         weave(nc.vector.tensor_copy, wb_woven0, wb_raw[0], 0, HALF)
         wb_q0 = quantise(nc, keep, wb_woven0, HALF, "wb0")
         wb_woven1 = woven_tile("wb_woven1", "wb_raw0")

@@ -26,10 +26,10 @@ def weave(copy, dst, src, c0, c1):
     copy(dst[:, c0:c1, :].rearrange("p (c i) t -> p c t i", i=4), src[:, :, c0:c1].rearrange("p t (c i) -> p c t i", i=4))
 
 
-def quantise(nc, pool, woven, width, name):
+def quantise(nc, pool, woven, width, name, first=0):
     codes = pool.tile([P, width], U32, name=name + "_codes", align_bytes=64)
     scales = pool.tile([P, width], U8, name=name + "_scales", align_bytes=64)
-    nc.vector.quantize_mx(out=codes[:].bitcast(FP8X4), scales=scales[:], in_=woven[:].rearrange("p c t -> p (c t)"))
+    nc.vector.quantize_mx(out=codes[:].bitcast(FP8X4), scales=scales[:], in_=woven[:, first : first + width, :].rearrange("p c t -> p (c t)"))
     return codes, scales
 
 
@@ -44,7 +44,7 @@ def tile_picked_gramsel_none_p_kernel(tc, x_words, x_scales, wa, wb, gt, gi, off
         fa_sb = lists.tile([P, V // 16], U16, name="fa_sb")
         xw = keep.tile([P, T], U32, name="xw", align_bytes=64)
         xs = keep.tile([P, T], U8, name="xs", align_bytes=64)
-        gt_sb = keep.tile([P, PACK], F32, name="gt_sb")
+        gt_sb = [keep.tile([P, PACK], F32, name="gt_sb%d" % h, tag="gt_sb%d" % h, align_bytes=64) for h in range(2)]
         gi_sb = keep.tile([P, PACK], F32, name="gi_sb", tag="after_a", align_bytes=64)
 
         def load_half(w, h, name):
@@ -64,7 +64,8 @@ def tile_picked_gramsel_none_p_kernel(tc, x_words, x_scales, wa, wb, gt, gi, off
         wb_raw = [load_half(wb, 0, "wb_raw0")]
         nc.sync.dma_start(fa_sb[:], fa)
         wb_raw.append(load_half(wb, 1, "wb_raw1"))
-        nc.sync.dma_start(gt_sb[:], gt.rearrange("(p t) o -> p (t o)", t=PACK))
+        for h in range(2):
+            nc.sync.dma_start(gt_sb[h][:], gt.rearrange("(p t) o -> p (t o)", t=PACK))
 
         nc.vector.memset(xs[:].bitcast(I32), 0)
         for q in range(4):
@@ -77,10 +78,10 @@ def tile_picked_gramsel_none_p_kernel(tc, x_words, x_scales, wa, wb, gt, gi, off
 
         xq_codes = keep.tile([P, S], U32, name="xq_codes", align_bytes=64)
         nc.vector.tensor_copy(xq_codes[:].rearrange("p (t m) -> p m t", t=PACK), xw[:].indirect(offs_sb[:]))
-        xq_scales = keep.tile([P, S], U8, name="xq_scales", align_bytes=64)
-        nc.vector.tensor_copy(xq_scales[:].rearrange("p (t m) -> p t m", t=PACK), sg[:].rearrange("p (m t) -> p t m", t=PACK))
         wa_woven0 = woven_tile("wa_woven0", "wa_woven0")
         weave(nc.scalar.copy, wa_woven0, wa_raw0, 0, HALF)
+        xq_scales = keep.tile([P, S], U8, name="xq_scales", align_bytes=64)
+        nc.vector.tensor_copy(xq_scales[:].rearrange("p (t m) -> p t m", t=PACK), sg[:].rearrange("p (m t) -> p t m", t=PACK))
         wa_q0 = quantise(nc, keep, wa_woven0, HALF, "wa0")
 
         def project(t, quantised, bank):
@@ -111,11 +112,11 @@ def tile_picked_gramsel_none_p_kernel(tc, x_words, x_scales, wa, wb, gt, gi, off
         def look_up(t):
             nc.vector.tensor_copy(z2_planes[:, t, :], a_rows[t][:].indirect(fa_sb[:]))
 
-        def z_half(quantised, first_bank, name, tag):
+        def z_half(quantised, factors, first_bank, name, tag):
             planes = keep.tile([P, PACK, HALF], BF16, name=name, tag=tag, align_bytes=64)
             for t in range(PACK):
                 sums = project(t, quantised, first_bank + t)
-                nc.scalar.activation(planes[:, t, :], sums[:], COPY, scale=gt_sb[:, t : t + 1])
+                nc.scalar.activation(planes[:, t, :], sums[:], COPY, scale=factors[:, t : t + 1])
             return planes
 
         wb_woven0 = woven_tile("wb_woven0", "wa_raw1")
@@ -127,21 +128,36 @@ def tile_picked_gramsel_none_p_kernel(tc, x_words, x_scales, wa, wb, gt, gi, off
         wb_q1 = quantise(nc, keep, wb_woven1, HALF, "wb1")
         for t in range(1, PACK):
             look_up(t)
-        z_planes0 = z_half(wb_q0, 0, "z_planes0", "after_a")
-        z_planes1 = z_half(wb_q1, PACK, "z_planes1", "z_planes1")
+        z_planes0 = z_half(wb_q0, gt_sb[0], 0, "z_planes0", "after_a")
+        z_planes1 = z_half(wb_q1, gt_sb[1], PACK, "z_planes1", "z_planes1")
+        for u in range(2):
+            spare = psum.tile([P, S], F32, name="spare", tag="bank%d" % (PACK + 0 + u))
+            nc.tensor.matmul_mx(
+                out=spare[:],
+                lhsT=xq_codes[:, 0:P].bitcast(FP8X4),
+                lhsT_scale=xq_scales[:, 0:P],
+                rhs=xq_codes[:].bitcast(FP8X4),
+                rhs_scale=xq_scales[:],
+                start=True,
+                stop=True,
+            )
         z_woven0 = woven_tile("z_woven0", "z_woven0")
         weave(nc.vector.tensor_copy, z_woven0, z_planes0, 0, HALF)
-        z2_woven = woven_tile("z2_woven", "after_a")
+        z2_woven = woven_tile("z2_woven", "gt_sb0")
         weave(nc.vector.tensor_copy, z2_woven, z2_planes, 0, V)
         z_woven1 = woven_tile("z_woven1", "z_woven1")
         weave(nc.scalar.copy, z_woven1, z_planes1, 0, HALF)
         z_q0 = quantise(nc, keep, z_woven0, HALF, "zhalf0")
         z2_codes, z2_scales = quantise(nc, keep, z2_woven, V, "z2")
-        z_q1 = quantise(nc, keep, z_woven1, HALF, "zhalf1")
+        z_q1 = [quantise(nc, keep, z_woven1, CHUNK, "zchunk%d" % u, u * CHUNK) for u in range(2)]
 
         for c in range(H // CHUNK):
-            codes, scales = z_q1 if c // 2 else z_q0
-            cols = slice((c % 2) * CHUNK, (c % 2 + 1) * CHUNK)
+            if c // 2:
+                codes, scales = z_q1[c % 2]
+                cols = slice(0, CHUNK)
+            else:
+                codes, scales = z_q0
+                cols = slice(c * CHUNK, (c + 1) * CHUNK)
             bank = psum.tile([P, V], F32, name="out_bank", tag="bank%d" % c)
             nc.tensor.matmul_mx(
                 out=bank[:],
@@ -152,7 +168,7 @@ def tile_picked_gramsel_none_p_kernel(tc, x_words, x_scales, wa, wb, gt, gi, off
                 start=True,
                 stop=True,
             )
-            result = keep.tile([P, V], F32, name="result%d" % c)
+            result = keep.tile([P, V], F32, name="result%d" % c, tag="z_woven1" if c == 1 else "result%d" % c, align_bytes=64)
             if c % 2:
                 nc.vector.tensor_scalar(result[:], bank[:], 0.0625, None, MULT)
             else:

@@ -38,6 +38,7 @@ def tile_picked_gramsel_none_p_kernel(tc, x_words, x_scales, wa, wb, gt, gi, off
     with ExitStack() as ctx:
         lists = ctx.enter_context(tc.tile_pool(name="lists", bufs=1))
         keep = ctx.enter_context(tc.tile_pool(name="keep", bufs=1))
+        shared = ctx.enter_context(tc.tile_pool(name="shared", bufs=1))
         psum = ctx.enter_context(tc.psum_pool(name="psum", bufs=1))
 
         offs_sb = lists.tile([P, S // 16], U16, name="offs_sb")
@@ -62,8 +63,8 @@ def tile_picked_gramsel_none_p_kernel(tc, x_words, x_scales, wa, wb, gt, gi, off
         wa_raw1 = load_half(wa, 1, "wa_raw1")
         nc.sync.dma_start(gi_sb[:], gi.rearrange("(p t) o -> p (t o)", t=PACK))
         wb_raw = [load_half(wb, 0, "wb_raw0")]
-        nc.sync.dma_start(fa_sb[:], fa)
         wb_raw.append(load_half(wb, 1, "wb_raw1"))
+        nc.sync.dma_start(fa_sb[:], fa)
         for h in range(2):
             nc.sync.dma_start(gt_sb[h][:], gt.rearrange("(p t) o -> p (t o)", t=PACK))
 
@@ -103,8 +104,8 @@ def tile_picked_gramsel_none_p_kernel(tc, x_words, x_scales, wa, wb, gt, gi, off
         weave(nc.vector.tensor_copy, wa_woven1, wa_raw1, 0, 144)
         wa_q1 = quantise(nc, keep, wa_woven1, HALF, "wa1")
         a_rows = [keep.tile([P, H], F32, name="a_rows%d" % t) for t in range(PACK)]
-        for h, t in ((0, 0), (0, 1), (1, 0), (0, 2), (1, 1), (0, 3), (1, 2), (1, 3)):
-            sums = project(t, wa_q1 if h else wa_q0, PACK * h + t)
+        for h, t, bank in ((0, 0, 0), (0, 1, 1), (1, 0, 4), (1, 1, 5), (0, 2, 1), (0, 3, 4), (1, 2, 6), (1, 3, 7)):
+            sums = project(t, wa_q1 if h else wa_q0, bank)
             nc.scalar.activation(a_rows[t][:, h * HALF : (h + 1) * HALF], sums[:], COPY, scale=gi_sb[:, t : t + 1])
 
         z2_planes = keep.tile([P, PACK, V], BF16, name="z2_planes", align_bytes=64)
@@ -112,10 +113,9 @@ def tile_picked_gramsel_none_p_kernel(tc, x_words, x_scales, wa, wb, gt, gi, off
         def look_up(t):
             nc.vector.tensor_copy(z2_planes[:, t, :], a_rows[t][:].indirect(fa_sb[:]))
 
-        def z_half(quantised, factors, first_bank, name, tag):
-            planes = keep.tile([P, PACK, HALF], BF16, name=name, tag=tag, align_bytes=64)
+        def z_half(quantised, factors, banks, planes):
             for t in range(PACK):
-                sums = project(t, quantised, first_bank + t)
+                sums = project(t, quantised, banks[t])
                 nc.scalar.activation(planes[:, t, :], sums[:], COPY, scale=factors[:, t : t + 1])
             return planes
 
@@ -128,49 +128,57 @@ def tile_picked_gramsel_none_p_kernel(tc, x_words, x_scales, wa, wb, gt, gi, off
         wb_q1 = quantise(nc, keep, wb_woven1, HALF, "wb1")
         for t in range(1, PACK):
             look_up(t)
-        z_planes0 = z_half(wb_q0, gt_sb[0], 0, "z_planes0", "after_a")
-        z_planes1 = z_half(wb_q1, gt_sb[1], PACK, "z_planes1", "z_planes1")
-        for u in range(2):
-            spare = psum.tile([P, S], F32, name="spare", tag="bank%d" % (PACK + 0 + u))
-            nc.tensor.matmul_mx(
-                out=spare[:],
-                lhsT=xq_codes[:, 0:P].bitcast(FP8X4),
-                lhsT_scale=xq_scales[:, 0:P],
-                rhs=xq_codes[:].bitcast(FP8X4),
-                rhs_scale=xq_scales[:],
-                start=True,
-                stop=True,
-            )
-        z_woven0 = woven_tile("z_woven0", "z_woven0")
-        weave(nc.vector.tensor_copy, z_woven0, z_planes0, 0, HALF)
+        z_planes0 = z_half(wb_q0, gt_sb[0], (2, 3, 0, 5), keep.tile([P, PACK, HALF], BF16, name="z_planes0", tag="after_a", align_bytes=64))
+        z_planes1 = z_half(wb_q1, gt_sb[1], (1, 4, 6, 7), shared.tile([P, PACK, HALF], BF16, name="z_planes1", offset=0, align_bytes=64))
+        z_woven = [keep.tile([P, CHUNK, PACK], BF16, name="z_woven%d" % c, tag="z_woven%d" % c, align_bytes=64) for c in range(H // CHUNK)]
+
+        def weave_chunk(copy, c):
+            planes = z_planes1 if c // 2 else z_planes0
+            weave(copy, z_woven[c], planes[:, :, c % 2 * CHUNK : (c % 2 + 1) * CHUNK], 0, CHUNK)
+
+        def quantise_chunk(c):
+            return quantise(nc, keep, z_woven[c], CHUNK, "zchunk%d" % c)
+
+        weave_chunk(nc.scalar.copy, 2)
+        weave_chunk(nc.scalar.copy, 3)
+        weave_chunk(nc.vector.tensor_copy, 0)
         z2_woven = woven_tile("z2_woven", "gt_sb0")
         weave(nc.vector.tensor_copy, z2_woven, z2_planes, 0, V)
-        z_woven1 = woven_tile("z_woven1", "z_woven1")
-        weave(nc.scalar.copy, z_woven1, z_planes1, 0, HALF)
-        z_q0 = quantise(nc, keep, z_woven0, HALF, "zhalf0")
+        z_q = {0: quantise_chunk(0)}
         z2_codes, z2_scales = quantise(nc, keep, z2_woven, V, "z2")
-        z_q1 = [quantise(nc, keep, z_woven1, CHUNK, "zchunk%d" % u, u * CHUNK) for u in range(2)]
+        weave_chunk(nc.vector.tensor_copy, 1)
+        order = (0, 2, 1, 3)
+        for c in order[1:]:
+            z_q[c] = quantise_chunk(c)
 
-        for c in range(H // CHUNK):
-            if c // 2:
-                codes, scales = z_q1[c % 2]
-                cols = slice(0, CHUNK)
-            else:
-                codes, scales = z_q0
-                cols = slice(c * CHUNK, (c + 1) * CHUNK)
-            bank = psum.tile([P, V], F32, name="out_bank", tag="bank%d" % c)
+        def product(c, cols, bank):
+            codes, scales = z_q[c]
+            sums = psum.tile([P, cols.stop - cols.start], F32, name="out_sums", tag="bank%d" % bank)
             nc.tensor.matmul_mx(
-                out=bank[:],
-                lhsT=codes[:, cols].bitcast(FP8X4),
-                lhsT_scale=scales[:, cols],
-                rhs=z2_codes[:].bitcast(FP8X4),
-                rhs_scale=z2_scales[:],
+                out=sums[:],
+                lhsT=codes[:].bitcast(FP8X4),
+                lhsT_scale=scales[:],
+                rhs=z2_codes[:, cols].bitcast(FP8X4),
+                rhs_scale=z2_scales[:, cols],
                 start=True,
                 stop=True,
             )
-            result = keep.tile([P, V], F32, name="result%d" % c, tag="z_woven1" if c == 1 else "result%d" % c, align_bytes=64)
-            if c % 2:
-                nc.vector.tensor_scalar(result[:], bank[:], 0.0625, None, MULT)
+            return sums
+
+        def on_vector(dst, sums):
+            nc.vector.tensor_scalar(dst, sums[:], 0.0625, None, MULT)
+
+        def on_scalar(dst, sums):
+            nc.scalar.activation(dst, sums[:], COPY, scale=0.0625)
+
+        for c in order:
+            if c // 2:
+                result = keep.tile([P, V], F32, name="result%d" % c, align_bytes=64)
             else:
-                nc.scalar.activation(result[:], bank[:], COPY, scale=0.0625)
+                result = shared.tile([P, V], F32, name="result%d" % c, offset=4 * V * c, align_bytes=64)
+            if c == order[-1]:
+                for cols, bank, empty in ((slice(0, V // 2), 5, on_vector), (slice(V // 2, V), 1, on_scalar)):
+                    empty(result[:, cols], product(c, cols, bank))
+            else:
+                (on_vector if c == 1 else on_scalar)(result[:], product(c, slice(0, V), (2, 3, 0)[c]))
             nc.sync.dma_start(out[c * CHUNK : (c + 1) * CHUNK, :], result[:])

@@ -53,14 +53,14 @@ def tile_picked_gramsel_none_p_kernel(tc, x_words, x_scales, wa, wb, gt, gi, off
             nc.sync.dma_start(raw[:], w[:, h * HALF : (h + 1) * HALF].rearrange("(p t) c -> p t c", t=PACK))
             return raw
 
-        xs_rows = keep.tile([P, T], U8, name="xs_rows", align_bytes=64)
-        for q in range(4):
-            queue = nc.sync if q % 2 == 0 else nc.scalar
-            queue.dma_start(xs_rows[32 * q : 32 * q + 4, :].bitcast(I32), x_scales[0, 4 * q : 4 * q + 4, :].bitcast(I32))
+        nc.vector.memset(xs[:].bitcast(I32), 0)
         nc.sync.dma_start(offs_sb[:], offs)
-        nc.sync.dma_start(xw[:].bitcast(I32), x_words[0].rearrange("p n t -> p (n t)").bitcast(I32))
         wa_raw0 = load_half(wa, 0, "wa_raw0")
-        wa_raw1 = load_half(wa, 1, "wa_raw1")
+        for q in range(4):
+            nc.sync.dma_start(xs[32 * q : 32 * q + 4, :].bitcast(I32), x_scales[0, 4 * q : 4 * q + 4, :].bitcast(I32))
+        nc.sync.dma_start(xw[:].bitcast(I32), x_words[0].rearrange("p n t -> p (n t)").bitcast(I32))
+        wa_raw1 = shared.tile([P, PACK, HALF], F32, name="wa_raw1", offset=8 * HALF, align_bytes=64)
+        nc.sync.dma_start(wa_raw1[:], wa[:, HALF:].rearrange("(p t) c -> p t c", t=PACK))
         nc.sync.dma_start(gi_sb[:], gi.rearrange("(p t) o -> p (t o)", t=PACK))
         wb_raw = [load_half(wb, 0, "wb_raw0")]
         wb_raw.append(load_half(wb, 1, "wb_raw1"))
@@ -68,22 +68,19 @@ def tile_picked_gramsel_none_p_kernel(tc, x_words, x_scales, wa, wb, gt, gi, off
         for h in range(2):
             nc.sync.dma_start(gt_sb[h][:], gt.rearrange("(p t) o -> p (t o)", t=PACK))
 
-        nc.vector.memset(xs[:].bitcast(I32), 0)
-        for q in range(4):
-            nc.vector.tensor_copy(xs[32 * q : 32 * q + 4, :].bitcast(I32), xs_rows[32 * q : 32 * q + 4, :].bitcast(I32))
         sg = keep.tile([P, S], U8, name="sg", align_bytes=64)
         nc.vector.tensor_copy(sg[:], xs[:].indirect(offs_sb[:]))
 
         def woven_tile(name, tag):
             return keep.tile([P, HALF, PACK], BF16, name=name, tag=tag, align_bytes=64)
 
-        xq_codes = keep.tile([P, S], U32, name="xq_codes", align_bytes=64)
-        nc.vector.tensor_copy(xq_codes[:].rearrange("p (t m) -> p m t", t=PACK), xw[:].indirect(offs_sb[:]))
         wa_woven0 = woven_tile("wa_woven0", "wa_woven0")
         weave(nc.scalar.copy, wa_woven0, wa_raw0, 0, HALF)
-        xq_scales = keep.tile([P, S], U8, name="xq_scales", align_bytes=64)
-        nc.vector.tensor_copy(xq_scales[:].rearrange("p (t m) -> p t m", t=PACK), sg[:].rearrange("p (m t) -> p t m", t=PACK))
         wa_q0 = quantise(nc, keep, wa_woven0, HALF, "wa0")
+        xq_scales = keep.tile([P, S], U8, name="xq_scales", tag="wa_raw0", align_bytes=64)
+        nc.vector.tensor_copy(xq_scales[:].rearrange("p (t m) -> p t m", t=PACK), sg[:].rearrange("p (m t) -> p t m", t=PACK))
+        xq_codes = keep.tile([P, S], U32, name="xq_codes", tag="wa_woven0", align_bytes=64)
+        nc.vector.tensor_copy(xq_codes[:].rearrange("p (t m) -> p m t", t=PACK), xw[:].indirect(offs_sb[:]))
 
         def project(t, quantised, bank):
             codes, scales = quantised
@@ -100,10 +97,11 @@ def tile_picked_gramsel_none_p_kernel(tc, x_words, x_scales, wa, wb, gt, gi, off
             return sums
 
         wa_woven1 = woven_tile("wa_woven1", "after_wa")
-        weave(nc.scalar.copy, wa_woven1, wa_raw1, 144, HALF)
-        weave(nc.vector.tensor_copy, wa_woven1, wa_raw1, 0, 144)
+        weave(nc.scalar.copy, wa_woven1, wa_raw1, 128, HALF)
+        weave(nc.vector.tensor_copy, wa_woven1, wa_raw1, 0, 128)
         wa_q1 = quantise(nc, keep, wa_woven1, HALF, "wa1")
-        a_rows = [keep.tile([P, H], F32, name="a_rows%d" % t) for t in range(PACK)]
+        a_rows = [shared.tile([P, H], F32, name="a_rows0", offset=8 * HALF, align_bytes=64)]
+        a_rows.extend(keep.tile([P, H], F32, name="a_rows%d" % t) for t in range(1, PACK))
         for h, t, bank in ((0, 0, 0), (0, 1, 1), (1, 0, 4), (1, 1, 5), (0, 2, 1), (0, 3, 4), (1, 2, 6), (1, 3, 7)):
             sums = project(t, wa_q1 if h else wa_q0, bank)
             nc.scalar.activation(a_rows[t][:, h * HALF : (h + 1) * HALF], sums[:], COPY, scale=gi_sb[:, t : t + 1])
@@ -119,9 +117,15 @@ def tile_picked_gramsel_none_p_kernel(tc, x_words, x_scales, wa, wb, gt, gi, off
                 nc.scalar.activation(planes[:, t, :], sums[:], COPY, scale=factors[:, t : t + 1])
             return planes
 
-        wb_woven0 = woven_tile("wb_woven0", "wa_raw1")
-        weave(nc.vector.tensor_copy, wb_woven0, wb_raw[0], 0, HALF)
-        wb_q0 = quantise(nc, keep, wb_woven0, HALF, "wb0")
+        wb_woven0 = shared.tile([P, HALF, PACK], BF16, name="wb_woven0", offset=16 * HALF, align_bytes=64)
+        wb_codes0 = keep.tile([P, HALF], U32, name="wb0_codes", align_bytes=64)
+        wb_scales0 = keep.tile([P, HALF], U8, name="wb0_scales", align_bytes=64)
+        for u in range(2):
+            weave(nc.vector.tensor_copy, wb_woven0, wb_raw[0], u * CHUNK, (u + 1) * CHUNK)
+        for u in range(2):
+            cols = slice(u * CHUNK, (u + 1) * CHUNK)
+            nc.vector.quantize_mx(out=wb_codes0[:, cols].bitcast(FP8X4), scales=wb_scales0[:, cols], in_=wb_woven0[:, cols, :].rearrange("p c t -> p (c t)"))
+        wb_q0 = (wb_codes0, wb_scales0)
         wb_woven1 = woven_tile("wb_woven1", "wb_raw0")
         weave(nc.vector.tensor_copy, wb_woven1, wb_raw[1], 0, HALF)
         look_up(0)
@@ -132,13 +136,14 @@ def tile_picked_gramsel_none_p_kernel(tc, x_words, x_scales, wa, wb, gt, gi, off
         z_planes1 = z_half(wb_q1, gt_sb[1], (1, 4, 6, 7), shared.tile([P, PACK, HALF], BF16, name="z_planes1", offset=0, align_bytes=64))
         z_woven = [keep.tile([P, CHUNK, PACK], BF16, name="z_woven%d" % c, tag="z_woven%d" % c, align_bytes=64) for c in range(H // CHUNK)]
 
-        def weave_chunk(copy, c):
+        def weave_chunk(copy, c, first=0, last=CHUNK):
             planes = z_planes1 if c // 2 else z_planes0
-            weave(copy, z_woven[c], planes[:, :, c % 2 * CHUNK : (c % 2 + 1) * CHUNK], 0, CHUNK)
+            weave(copy, z_woven[c], planes[:, :, c % 2 * CHUNK : (c % 2 + 1) * CHUNK], first, last)
 
         def quantise_chunk(c):
             return quantise(nc, keep, z_woven[c], CHUNK, "zchunk%d" % c)
 
+        weave_chunk(nc.scalar.copy, 1, 64, CHUNK)
         weave_chunk(nc.scalar.copy, 2)
         weave_chunk(nc.scalar.copy, 3)
         weave_chunk(nc.vector.tensor_copy, 0)
@@ -146,7 +151,7 @@ def tile_picked_gramsel_none_p_kernel(tc, x_words, x_scales, wa, wb, gt, gi, off
         weave(nc.vector.tensor_copy, z2_woven, z2_planes, 0, V)
         z_q = {0: quantise_chunk(0)}
         z2_codes, z2_scales = quantise(nc, keep, z2_woven, V, "z2")
-        weave_chunk(nc.vector.tensor_copy, 1)
+        weave_chunk(nc.vector.tensor_copy, 1, 0, 64)
         order = (0, 2, 1, 3)
         for c in order[1:]:
             z_q[c] = quantise_chunk(c)

@@ -59,8 +59,9 @@ def tile_picked_gramsel_none_p_kernel(tc, x_words, x_scales, wa, wb, gt, gi, off
         for q in range(4):
             nc.sync.dma_start(xs[32 * q : 32 * q + 4, :].bitcast(I32), x_scales[0, 4 * q : 4 * q + 4, :].bitcast(I32))
         nc.sync.dma_start(xw[:].bitcast(I32), x_words[0].rearrange("p n t -> p (n t)").bitcast(I32))
-        wa_raw1 = shared.tile([P, PACK, HALF], F32, name="wa_raw1", offset=8 * HALF, align_bytes=64)
-        nc.sync.dma_start(wa_raw1[:], wa[:, HALF:].rearrange("(p t) c -> p t c", t=PACK))
+        wa_raw1 = [shared.tile([P, PACK, CHUNK], F32, name="wa_raw1%d" % u, offset=8 * HALF * (1 + u), align_bytes=64) for u in range(2)]
+        for u in range(2):
+            nc.sync.dma_start(wa_raw1[u][:], wa[:, HALF + u * CHUNK : HALF + (u + 1) * CHUNK].rearrange("(p t) c -> p t c", t=PACK))
         nc.sync.dma_start(gi_sb[:], gi.rearrange("(p t) o -> p (t o)", t=PACK))
         wb_raw = [load_half(wb, 0, "wb_raw0")]
         wb_raw.append(load_half(wb, 1, "wb_raw1"))
@@ -82,11 +83,10 @@ def tile_picked_gramsel_none_p_kernel(tc, x_words, x_scales, wa, wb, gt, gi, off
         xq_codes = keep.tile([P, S], U32, name="xq_codes", tag="wa_woven0", align_bytes=64)
         nc.vector.tensor_copy(xq_codes[:].rearrange("p (t m) -> p m t", t=PACK), xw[:].indirect(offs_sb[:]))
 
-        def project(t, quantised, bank):
+        def project(t, quantised, sums):
             codes, scales = quantised
-            sums = psum.tile([P, HALF], F32, name="sums", tag="bank%d" % bank)
             nc.tensor.matmul_mx(
-                out=sums[:],
+                out=sums,
                 lhsT=xq_codes[:, t * P : (t + 1) * P].bitcast(FP8X4),
                 lhsT_scale=xq_scales[:, t * P : (t + 1) * P],
                 rhs=codes[:].bitcast(FP8X4),
@@ -94,17 +94,27 @@ def tile_picked_gramsel_none_p_kernel(tc, x_words, x_scales, wa, wb, gt, gi, off
                 start=True,
                 stop=True,
             )
-            return sums
 
         wa_woven1 = woven_tile("wa_woven1", "after_wa")
-        weave(nc.scalar.copy, wa_woven1, wa_raw1, 128, HALF)
-        weave(nc.vector.tensor_copy, wa_woven1, wa_raw1, 0, 128)
-        wa_q1 = quantise(nc, keep, wa_woven1, HALF, "wa1")
+        weave(nc.scalar.copy, wa_woven1[:, :CHUNK, :], wa_raw1[0], 0, CHUNK)
+        weave(nc.vector.tensor_copy, wa_woven1[:, CHUNK:, :], wa_raw1[1], 0, CHUNK)
+        wa_codes1 = keep.tile([P, HALF], U32, name="wa1_codes", align_bytes=64)
+        wa_scales1 = keep.tile([P, HALF], U8, name="wa1_scales", align_bytes=64)
+        for u in range(2):
+            cols = slice(u * CHUNK, (u + 1) * CHUNK)
+            nc.vector.quantize_mx(out=wa_codes1[:, cols].bitcast(FP8X4), scales=wa_scales1[:, cols], in_=wa_woven1[:, cols, :].rearrange("p c t -> p (c t)"))
+        wa_q1 = (wa_codes1, wa_scales1)
         a_rows = [shared.tile([P, H], F32, name="a_rows0", offset=8 * HALF, align_bytes=64)]
         a_rows.extend(keep.tile([P, H], F32, name="a_rows%d" % t) for t in range(1, PACK))
-        for h, t, bank in ((0, 0, 0), (0, 1, 1), (1, 0, 4), (1, 1, 5), (0, 2, 1), (0, 3, 4), (1, 2, 6), (1, 3, 7)):
-            sums = project(t, wa_q1 if h else wa_q0, bank)
+        for h, t, bank in ((0, 0, 0), (0, 1, 1), (1, 0, 4), (1, 1, 5)):
+            sums = psum.tile([P, HALF], F32, name="sums", tag="bank%d" % bank)
+            project(t, wa_q1 if h else wa_q0, sums[:])
             nc.scalar.activation(a_rows[t][:, h * HALF : (h + 1) * HALF], sums[:], COPY, scale=gi_sb[:, t : t + 1])
+        for t, bank in ((2, 0), (3, 1)):
+            sums = psum.tile([P, H], F32, name="sums", tag="bank%d" % bank)
+            for h, quantised in enumerate((wa_q0, wa_q1)):
+                project(t, quantised, sums[:, h * HALF : (h + 1) * HALF])
+            nc.scalar.activation(a_rows[t][:], sums[:], COPY, scale=gi_sb[:, t : t + 1])
 
         z2_planes = keep.tile([P, PACK, V], BF16, name="z2_planes", align_bytes=64)
 
@@ -113,7 +123,8 @@ def tile_picked_gramsel_none_p_kernel(tc, x_words, x_scales, wa, wb, gt, gi, off
 
         def z_half(quantised, factors, banks, planes):
             for t in range(PACK):
-                sums = project(t, quantised, banks[t])
+                sums = psum.tile([P, HALF], F32, name="sums", tag="bank%d" % banks[t])
+                project(t, quantised, sums[:])
                 nc.scalar.activation(planes[:, t, :], sums[:], COPY, scale=factors[:, t : t + 1])
             return planes
 
@@ -132,8 +143,8 @@ def tile_picked_gramsel_none_p_kernel(tc, x_words, x_scales, wa, wb, gt, gi, off
         wb_q1 = quantise(nc, keep, wb_woven1, HALF, "wb1")
         for t in range(1, PACK):
             look_up(t)
-        z_planes0 = z_half(wb_q0, gt_sb[0], (2, 3, 0, 5), keep.tile([P, PACK, HALF], BF16, name="z_planes0", tag="after_a", align_bytes=64))
-        z_planes1 = z_half(wb_q1, gt_sb[1], (1, 4, 6, 7), shared.tile([P, PACK, HALF], BF16, name="z_planes1", offset=0, align_bytes=64))
+        z_planes0 = z_half(wb_q0, gt_sb[0], (2, 3, 6, 7), keep.tile([P, PACK, HALF], BF16, name="z_planes0", tag="after_a", align_bytes=64))
+        z_planes1 = z_half(wb_q1, gt_sb[1], (4, 5, 0, 1), shared.tile([P, PACK, HALF], BF16, name="z_planes1", offset=0, align_bytes=64))
         z_woven = [keep.tile([P, CHUNK, PACK], BF16, name="z_woven%d" % c, tag="z_woven%d" % c, align_bytes=64) for c in range(H // CHUNK)]
 
         def weave_chunk(copy, c, first=0, last=CHUNK):
@@ -182,8 +193,8 @@ def tile_picked_gramsel_none_p_kernel(tc, x_words, x_scales, wa, wb, gt, gi, off
             else:
                 result = shared.tile([P, V], F32, name="result%d" % c, offset=4 * V * c, align_bytes=64)
             if c == order[-1]:
-                for cols, bank, empty in ((slice(0, V // 2), 5, on_vector), (slice(V // 2, V), 1, on_scalar)):
+                for cols, bank, empty in ((slice(0, V // 2), 7, on_vector), (slice(V // 2, V), 4, on_scalar)):
                     empty(result[:, cols], product(c, cols, bank))
             else:
-                (on_vector if c == 1 else on_scalar)(result[:], product(c, slice(0, V), (2, 3, 0)[c]))
+                (on_vector if c == 1 else on_scalar)(result[:], product(c, slice(0, V), (2, 3, 6)[c]))
             nc.sync.dma_start(out[c * CHUNK : (c + 1) * CHUNK, :], result[:])

@@ -59,9 +59,9 @@ def tile_picked_gramsel_none_p_kernel(tc, x_words, x_scales, wa, wb, gt, gi, off
         for q in range(4):
             nc.sync.dma_start(xs[32 * q : 32 * q + 4, :].bitcast(I32), x_scales[0, 4 * q : 4 * q + 4, :].bitcast(I32))
         nc.sync.dma_start(xw[:].bitcast(I32), x_words[0].rearrange("p n t -> p (n t)").bitcast(I32))
-        wa_raw1 = [shared.tile([P, PACK, CHUNK], F32, name="wa_raw1%d" % u, offset=8 * HALF * (1 + u), align_bytes=64) for u in range(2)]
+        wa_raw1 = [shared.tile([P, 2, HALF], F32, name="wa_raw1%d" % u, offset=8 * HALF * (1 + u), align_bytes=64) for u in range(2)]
         for u in range(2):
-            nc.sync.dma_start(wa_raw1[u][:], wa[:, HALF + u * CHUNK : HALF + (u + 1) * CHUNK].rearrange("(p t) c -> p t c", t=PACK))
+            nc.sync.dma_start(wa_raw1[u][:], wa[:, HALF:].rearrange("(p t) c -> p t c", t=PACK)[:, 2 * u : 2 * u + 2, :])
         nc.sync.dma_start(gi_sb[:], gi.rearrange("(p t) o -> p (t o)", t=PACK))
         wb_raw = [load_half(wb, 0, "wb_raw0")]
         wb_raw.append(load_half(wb, 1, "wb_raw1"))
@@ -96,8 +96,9 @@ def tile_picked_gramsel_none_p_kernel(tc, x_words, x_scales, wa, wb, gt, gi, off
             )
 
         wa_woven1 = woven_tile("wa_woven1", "after_wa")
-        weave(nc.scalar.copy, wa_woven1[:, :CHUNK, :], wa_raw1[0], 0, CHUNK)
-        weave(nc.vector.tensor_copy, wa_woven1[:, CHUNK:, :], wa_raw1[1], 0, CHUNK)
+        weave(nc.scalar.copy, wa_woven1[:, :, :2], wa_raw1[0], 0, HALF)
+        for u in range(2):
+            weave(nc.vector.tensor_copy, wa_woven1[:, :, 2:], wa_raw1[1], u * CHUNK, (u + 1) * CHUNK)
         wa_codes1 = keep.tile([P, HALF], U32, name="wa1_codes", align_bytes=64)
         wa_scales1 = keep.tile([P, HALF], U8, name="wa1_scales", align_bytes=64)
         for u in range(2):

@@ -69,14 +69,14 @@ def tile_picked_gramsel_none_p_kernel(tc, x_words, x_scales, wa, wb, gt, gi, off
         for h in range(2):
             nc.sync.dma_start(gt_sb[h][:], gt.rearrange("(p t) o -> p (t o)", t=PACK))
 
-        sg = keep.tile([P, S], U8, name="sg", align_bytes=64)
-        nc.vector.tensor_copy(sg[:], xs[:].indirect(offs_sb[:]))
-
         def woven_tile(name, tag):
             return keep.tile([P, HALF, PACK], BF16, name=name, tag=tag, align_bytes=64)
 
         wa_woven0 = woven_tile("wa_woven0", "wa_woven0")
-        weave(nc.scalar.copy, wa_woven0, wa_raw0, 0, HALF)
+        weave(nc.vector.tensor_copy, wa_woven0, wa_raw0, 0, 64)
+        weave(nc.scalar.copy, wa_woven0, wa_raw0, 64, HALF)
+        sg = keep.tile([P, S], U8, name="sg", align_bytes=64)
+        nc.vector.tensor_copy(sg[:], xs[:].indirect(offs_sb[:]))
         wa_q0 = quantise(nc, keep, wa_woven0, HALF, "wa0")
         xq_scales = keep.tile([P, S], U8, name="xq_scales", tag="wa_raw0", align_bytes=64)
         nc.vector.tensor_copy(xq_scales[:].rearrange("p (t m) -> p t m", t=PACK), sg[:].rearrange("p (m t) -> p t m", t=PACK))

@@ -14,23 +14,20 @@ U8 = mybir.dt.uint8
 FP8X4 = mybir.dt.float8_e4m3fn_x4
 COPY = mybir.ActivationFunctionType.Copy
 MULT = mybir.AluOpType.mult
-ADD = mybir.AluOpType.add
 
 P = 128
 PACK = 4
 HALF = 256
 CHUNK = 128
+WA0_VECTOR = 64
 
 
 def weave(copy, dst, src, c0, c1):
     copy(dst[:, c0:c1, :].rearrange("p (c i) t -> p c t i", i=4), src[:, :, c0:c1].rearrange("p t (c i) -> p c t i", i=4))
 
 
-def quantise(nc, pool, woven, width, name, first=0):
-    codes = pool.tile([P, width], U32, name=name + "_codes", align_bytes=64)
-    scales = pool.tile([P, width], U8, name=name + "_scales", align_bytes=64)
-    nc.vector.quantize_mx(out=codes[:].bitcast(FP8X4), scales=scales[:], in_=woven[:, first : first + width, :].rearrange("p c t -> p (c t)"))
-    return codes, scales
+def quantise(nc, codes, scales, woven, c0, c1):
+    nc.vector.quantize_mx(out=codes[:, c0:c1].bitcast(FP8X4), scales=scales[:, c0:c1], in_=woven[:, c0:c1, :].rearrange("p c t -> p (c t)"))
 
 
 def tile_picked_gramsel_none_p_kernel(tc, x_words, x_scales, wa, wb, gt, gi, offs, fa, out):
@@ -38,20 +35,36 @@ def tile_picked_gramsel_none_p_kernel(tc, x_words, x_scales, wa, wb, gt, gi, off
     with ExitStack() as ctx:
         lists = ctx.enter_context(tc.tile_pool(name="lists", bufs=1))
         keep = ctx.enter_context(tc.tile_pool(name="keep", bufs=1))
-        shared = ctx.enter_context(tc.tile_pool(name="shared", bufs=1))
         psum = ctx.enter_context(tc.psum_pool(name="psum", bufs=1))
+
+        def operand(name, width, tag=None):
+            codes = keep.tile([P, width], U32, name=name + "_codes", tag=tag or name + "_codes", align_bytes=64)
+            scales = keep.tile([P, width], U8, name=name + "_scales", align_bytes=64)
+            return codes, scales
+
+        def woven_tile(name, width, tag):
+            return keep.tile([P, width, PACK], BF16, name=name, tag=tag, align_bytes=64)
 
         offs_sb = lists.tile([P, S // 16], U16, name="offs_sb")
         fa_sb = lists.tile([P, V // 16], U16, name="fa_sb")
         xw = keep.tile([P, T], U32, name="xw", align_bytes=64)
         xs = keep.tile([P, T], U8, name="xs", align_bytes=64)
-        gt_sb = [keep.tile([P, PACK], F32, name="gt_sb%d" % h, tag="gt_sb%d" % h, align_bytes=64) for h in range(2)]
-        gi_sb = keep.tile([P, PACK], F32, name="gi_sb", tag="after_a", align_bytes=64)
+        gt_sb = keep.tile([P, PACK], F32, name="gt_sb", align_bytes=64)
+        gi_sb = keep.tile([P, PACK], F32, name="gi_sb", align_bytes=64)
+
+        def half_rows(w, h):
+            return w[:, h * HALF : (h + 1) * HALF].rearrange("(p t) c -> p t c", t=PACK)
 
         def load_half(w, h, name):
             raw = keep.tile([P, PACK, HALF], F32, name=name, tag=name, align_bytes=64)
-            nc.sync.dma_start(raw[:], w[:, h * HALF : (h + 1) * HALF].rearrange("(p t) c -> p t c", t=PACK))
+            nc.sync.dma_start(raw[:], half_rows(w, h))
             return raw
+
+        def load_pairs(w, h, name):
+            pairs = [keep.tile([P, 2, HALF], F32, name="%s%d" % (name, u), tag="%s%d" % (name, u), align_bytes=64) for u in range(2)]
+            for u in range(2):
+                nc.sync.dma_start(pairs[u][:], half_rows(w, h)[:, 2 * u : 2 * u + 2, :])
+            return pairs
 
         nc.vector.memset(xs[:].bitcast(I32), 0)
         nc.sync.dma_start(offs_sb[:], offs)
@@ -59,127 +72,97 @@ def tile_picked_gramsel_none_p_kernel(tc, x_words, x_scales, wa, wb, gt, gi, off
         for q in range(4):
             nc.sync.dma_start(xs[32 * q : 32 * q + 4, :].bitcast(I32), x_scales[0, 4 * q : 4 * q + 4, :].bitcast(I32))
         nc.sync.dma_start(xw[:].bitcast(I32), x_words[0].rearrange("p n t -> p (n t)").bitcast(I32))
-        wa_raw1 = [shared.tile([P, 2, HALF], F32, name="wa_raw1%d" % u, offset=8 * HALF * (1 + u), align_bytes=64) for u in range(2)]
-        for u in range(2):
-            nc.sync.dma_start(wa_raw1[u][:], wa[:, HALF:].rearrange("(p t) c -> p t c", t=PACK)[:, 2 * u : 2 * u + 2, :])
+        wa_raw1 = load_pairs(wa, 1, "wa_pair")
         nc.sync.dma_start(gi_sb[:], gi.rearrange("(p t) o -> p (t o)", t=PACK))
-        wb_raw = [load_half(wb, 0, "wb_raw0")]
-        wb_raw.append(load_half(wb, 1, "wb_raw1"))
+        wb_raw = [load_half(wb, h, "wb_raw%d" % h) for h in range(2)]
         nc.sync.dma_start(fa_sb[:], fa)
-        for h in range(2):
-            nc.sync.dma_start(gt_sb[h][:], gt.rearrange("(p t) o -> p (t o)", t=PACK))
+        nc.sync.dma_start(gt_sb[:], gt.rearrange("(p t) o -> p (t o)", t=PACK))
 
-        def woven_tile(name, tag):
-            return keep.tile([P, HALF, PACK], BF16, name=name, tag=tag, align_bytes=64)
-
-        wa_woven0 = woven_tile("wa_woven0", "wa_woven0")
-        weave(nc.vector.tensor_copy, wa_woven0, wa_raw0, 0, 64)
-        weave(nc.scalar.copy, wa_woven0, wa_raw0, 64, HALF)
-        sg = keep.tile([P, S], U8, name="sg", align_bytes=64)
-        nc.vector.tensor_copy(sg[:], xs[:].indirect(offs_sb[:]))
-        wa_q0 = quantise(nc, keep, wa_woven0, HALF, "wa0")
-        xq_scales = keep.tile([P, S], U8, name="xq_scales", tag="wa_raw0", align_bytes=64)
-        nc.vector.tensor_copy(xq_scales[:].rearrange("p (t m) -> p t m", t=PACK), sg[:].rearrange("p (m t) -> p t m", t=PACK))
+        wa_woven0 = woven_tile("wa_woven0", HALF, "wa_woven0")
+        weave(nc.vector.tensor_copy, wa_woven0, wa_raw0, 0, WA0_VECTOR)
+        weave(nc.scalar.copy, wa_woven0, wa_raw0, WA0_VECTOR, HALF)
+        xq_scales = keep.tile([P, S], U8, name="xq_scales", align_bytes=64)
+        nc.vector.tensor_copy(xq_scales[:].rearrange("p (t m) -> p m t", t=PACK), xs[:].indirect(offs_sb[:]))
+        wa_q = [operand("wa%d" % h, HALF) for h in range(2)]
+        quantise(nc, *wa_q[0], wa_woven0, 0, HALF)
         xq_codes = keep.tile([P, S], U32, name="xq_codes", tag="wa_woven0", align_bytes=64)
         nc.vector.tensor_copy(xq_codes[:].rearrange("p (t m) -> p m t", t=PACK), xw[:].indirect(offs_sb[:]))
 
-        def project(t, quantised, sums):
-            codes, scales = quantised
+        def multiply(sums, stationary, rows, moving, cols):
             nc.tensor.matmul_mx(
                 out=sums,
-                lhsT=xq_codes[:, t * P : (t + 1) * P].bitcast(FP8X4),
-                lhsT_scale=xq_scales[:, t * P : (t + 1) * P],
-                rhs=codes[:].bitcast(FP8X4),
-                rhs_scale=scales[:],
+                lhsT=stationary[0][:, rows].bitcast(FP8X4),
+                lhsT_scale=stationary[1][:, rows],
+                rhs=moving[0][:, cols].bitcast(FP8X4),
+                rhs_scale=moving[1][:, cols],
                 start=True,
                 stop=True,
             )
 
-        wa_woven1 = woven_tile("wa_woven1", "after_wa")
+        def project(t, weights, cols, sums):
+            multiply(sums, (xq_codes, xq_scales), slice(t * P, (t + 1) * P), weights, cols)
+
+        wa_woven1 = woven_tile("wa_woven1", HALF, "wa_woven1")
         weave(nc.scalar.copy, wa_woven1[:, :, :2], wa_raw1[0], 0, HALF)
         for u in range(2):
             weave(nc.vector.tensor_copy, wa_woven1[:, :, 2:], wa_raw1[1], u * CHUNK, (u + 1) * CHUNK)
-        wa_codes1 = keep.tile([P, HALF], U32, name="wa1_codes", align_bytes=64)
-        wa_scales1 = keep.tile([P, HALF], U8, name="wa1_scales", align_bytes=64)
         for u in range(2):
-            cols = slice(u * CHUNK, (u + 1) * CHUNK)
-            nc.vector.quantize_mx(out=wa_codes1[:, cols].bitcast(FP8X4), scales=wa_scales1[:, cols], in_=wa_woven1[:, cols, :].rearrange("p c t -> p (c t)"))
-        wa_q1 = (wa_codes1, wa_scales1)
-        a_rows = [shared.tile([P, H], F32, name="a_rows0", offset=8 * HALF, align_bytes=64)]
-        a_rows.extend(keep.tile([P, H], F32, name="a_rows%d" % t) for t in range(1, PACK))
-        for h, t, bank in ((0, 0, 0), (0, 1, 1), (1, 0, 4), (1, 1, 5)):
-            sums = psum.tile([P, HALF], F32, name="sums", tag="bank%d" % bank)
-            project(t, wa_q1 if h else wa_q0, sums[:])
-            nc.scalar.activation(a_rows[t][:, h * HALF : (h + 1) * HALF], sums[:], COPY, scale=gi_sb[:, t : t + 1])
-        for t, bank in ((2, 0), (3, 1)):
-            sums = psum.tile([P, H], F32, name="sums", tag="bank%d" % bank)
-            for h, quantised in enumerate((wa_q0, wa_q1)):
-                project(t, quantised, sums[:, h * HALF : (h + 1) * HALF])
-            nc.scalar.activation(a_rows[t][:], sums[:], COPY, scale=gi_sb[:, t : t + 1])
+            quantise(nc, *wa_q[1], wa_woven1, u * CHUNK, (u + 1) * CHUNK)
 
-        z2_planes = keep.tile([P, PACK, V], BF16, name="z2_planes", align_bytes=64)
-
-        def look_up(t):
-            nc.vector.tensor_copy(z2_planes[:, t, :], a_rows[t][:].indirect(fa_sb[:]))
-
-        def z_half(quantised, factors, banks, planes):
+        whole = slice(0, HALF)
+        a_rows = [keep.tile([P, H], F32, name="a_rows%d" % t, tag="wa_pair0" if t == 0 else "a_rows%d" % t, align_bytes=64) for t in range(PACK)]
+        for h in range(2):
             for t in range(PACK):
-                sums = psum.tile([P, HALF], F32, name="sums", tag="bank%d" % banks[t])
-                project(t, quantised, sums[:])
-                nc.scalar.activation(planes[:, t, :], sums[:], COPY, scale=factors[:, t : t + 1])
-            return planes
+                sums = psum.tile([P, HALF], F32, name="sums", tag="bank%d" % (0, 1, 4, 5)[t])
+                project(t, wa_q[h], whole, sums[:])
+                nc.scalar.activation(a_rows[t][:, h * HALF : (h + 1) * HALF], sums[:], COPY, scale=gi_sb[:, t : t + 1])
+        row = keep.tile([P, 2 * PACK * V], BF16, name="row", align_bytes=64)
+        z2_planes = row[:, : PACK * V].rearrange("p (t v) -> p t v", t=PACK)
+        z2_woven = row[:, PACK * V :].rearrange("p (v t) -> p v t", t=PACK)
+        for t in range(PACK - 1):
+            nc.scalar.activation(z2_planes[:, t, :], a_rows[t][:].indirect(fa_sb[:]), COPY)
 
-        wb_woven0 = shared.tile([P, HALF, PACK], BF16, name="wb_woven0", offset=16 * HALF, align_bytes=64)
-        wb_codes0 = keep.tile([P, HALF], U32, name="wb0_codes", align_bytes=64)
-        wb_scales0 = keep.tile([P, HALF], U8, name="wb0_scales", align_bytes=64)
-        for u in range(2):
-            weave(nc.vector.tensor_copy, wb_woven0, wb_raw[0], u * CHUNK, (u + 1) * CHUNK)
-        for u in range(2):
-            cols = slice(u * CHUNK, (u + 1) * CHUNK)
-            nc.vector.quantize_mx(out=wb_codes0[:, cols].bitcast(FP8X4), scales=wb_scales0[:, cols], in_=wb_woven0[:, cols, :].rearrange("p c t -> p (c t)"))
-        wb_q0 = (wb_codes0, wb_scales0)
-        wb_woven1 = woven_tile("wb_woven1", "wb_raw0")
-        weave(nc.vector.tensor_copy, wb_woven1, wb_raw[1], 0, HALF)
-        look_up(0)
-        wb_q1 = quantise(nc, keep, wb_woven1, HALF, "wb1")
-        for t in range(1, PACK):
-            look_up(t)
-        z_planes0 = z_half(wb_q0, gt_sb[0], (2, 3, 6, 7), keep.tile([P, PACK, HALF], BF16, name="z_planes0", tag="after_a", align_bytes=64))
-        z_planes1 = z_half(wb_q1, gt_sb[1], (4, 5, 0, 1), shared.tile([P, PACK, HALF], BF16, name="z_planes1", offset=0, align_bytes=64))
-        z_woven = [keep.tile([P, CHUNK, PACK], BF16, name="z_woven%d" % c, tag="z_woven%d" % c, align_bytes=64) for c in range(H // CHUNK)]
+        last_plane = (PACK - 1) * V
+        wb_woven = [woven_tile("wb_woven0", HALF, "wa_pair1"), row[:, last_plane : last_plane + PACK * HALF].rearrange("p (c t) -> p c t", t=PACK)]
+        wb_q = [operand("wb%d" % h, HALF) for h in range(2)]
+        z_woven = [woven_tile("z_woven0", HALF, "wb_raw1"), woven_tile("z_woven1", HALF, "z_woven1")]
+        z_q = [operand("zhalf%d" % h, HALF) for h in range(2)]
 
-        def weave_chunk(copy, c, first=0, last=CHUNK):
-            planes = z_planes1 if c // 2 else z_planes0
-            weave(copy, z_woven[c], planes[:, :, c % 2 * CHUNK : (c % 2 + 1) * CHUNK], first, last)
+        def chunk(c):
+            return slice(c % 2 * CHUNK, (c % 2 + 1) * CHUNK)
 
-        def quantise_chunk(c):
-            return quantise(nc, keep, z_woven[c], CHUNK, "zchunk%d" % c)
+        def project_chunk(c):
+            sums = psum.tile([P, PACK, CHUNK], F32, name="b_sums", tag="bank%d" % (2, 3, 6, 7)[c])
+            for t in range(PACK):
+                project(t, wb_q[c // 2], chunk(c), sums[:, t, :])
+            return sums
 
-        weave_chunk(nc.scalar.copy, 1, 64, CHUNK)
-        weave_chunk(nc.scalar.copy, 2)
-        weave_chunk(nc.scalar.copy, 3)
-        weave_chunk(nc.vector.tensor_copy, 0)
-        z2_woven = woven_tile("z2_woven", "gt_sb0")
+        def scale_chunk(c):
+            nc.vector.tensor_tensor(z_woven[c // 2][:, chunk(c), :], project_chunk(c)[:].rearrange("p t n -> p n t"), gt_sb[:].unsqueeze(1).to_broadcast([P, CHUNK, PACK]), MULT)
+
+        weave(nc.vector.tensor_copy, wb_woven[0], wb_raw[0], 0, HALF)
+        quantise(nc, *wb_q[0], wb_woven[0], 0, HALF)
+        weave(nc.vector.tensor_copy, wb_woven[1], wb_raw[1], 0, HALF)
+        scale_chunk(0)
+        quantise(nc, *wb_q[1], wb_woven[1], 0, HALF)
+        nc.vector.tensor_copy(z2_planes[:, PACK - 1, :], a_rows[PACK - 1][:].indirect(fa_sb[:]))
+        scale_chunk(1)
         weave(nc.vector.tensor_copy, z2_woven, z2_planes, 0, V)
-        z_q = {0: quantise_chunk(0)}
-        z2_codes, z2_scales = quantise(nc, keep, z2_woven, V, "z2")
-        weave_chunk(nc.vector.tensor_copy, 1, 0, 64)
-        order = (0, 2, 1, 3)
-        for c in order[1:]:
-            z_q[c] = quantise_chunk(c)
+        quantise(nc, *z_q[0], z_woven[0], 0, HALF)
+        z2_q = operand("z2", V)
+        quantise(nc, *z2_q, z2_woven, 0, V)
+        scale_chunk(2)
+        sums = project_chunk(3)
+        z_planes = keep.tile([P, PACK, CHUNK], BF16, name="z_planes", align_bytes=64)
+        for t in range(PACK):
+            nc.scalar.activation(z_planes[:, t, :], sums[:, t, :], COPY, scale=gt_sb[:, t : t + 1])
+        weave(nc.scalar.copy, z_woven[1][:, CHUNK:, :], z_planes, 0, CHUNK)
+        quantise(nc, *z_q[1], z_woven[1], CHUNK, HALF)
+        quantise(nc, *z_q[1], z_woven[1], 0, CHUNK)
 
         def product(c, cols, bank):
-            codes, scales = z_q[c]
             sums = psum.tile([P, cols.stop - cols.start], F32, name="out_sums", tag="bank%d" % bank)
-            nc.tensor.matmul_mx(
-                out=sums[:],
-                lhsT=codes[:].bitcast(FP8X4),
-                lhsT_scale=scales[:],
-                rhs=z2_codes[:, cols].bitcast(FP8X4),
-                rhs_scale=z2_scales[:, cols],
-                start=True,
-                stop=True,
-            )
+            multiply(sums[:], z_q[c // 2], chunk(c), z2_q, cols)
             return sums
 
         def on_vector(dst, sums):
@@ -188,14 +171,11 @@ def tile_picked_gramsel_none_p_kernel(tc, x_words, x_scales, wa, wb, gt, gi, off
         def on_scalar(dst, sums):
             nc.scalar.activation(dst, sums[:], COPY, scale=0.0625)
 
-        for c in order:
-            if c // 2:
-                result = keep.tile([P, V], F32, name="result%d" % c, align_bytes=64)
-            else:
-                result = shared.tile([P, V], F32, name="result%d" % c, offset=4 * V * c, align_bytes=64)
-            if c == order[-1]:
-                for cols, bank, empty in ((slice(0, V // 2), 7, on_vector), (slice(V // 2, V), 4, on_scalar)):
+        for c, banks in ((0, (4,)), (1, (5,)), (3, (0, 1)), (2, (2, 3))):
+            result = keep.tile([P, V], F32, name="result%d" % c, align_bytes=64)
+            if len(banks) == 2:
+                for cols, bank, empty in ((slice(0, V // 2), banks[0], on_vector), (slice(V // 2, V), banks[1], on_scalar)):
                     empty(result[:, cols], product(c, cols, bank))
             else:
-                (on_vector if c == 1 else on_scalar)(result[:], product(c, slice(0, V), (2, 3, 6)[c]))
+                on_scalar(result[:], product(c, slice(0, V), banks[0]))
             nc.sync.dma_start(out[c * CHUNK : (c + 1) * CHUNK, :], result[:])

@@ -119,10 +119,17 @@ def tile_picked_gramsel_none_p_kernel(tc, x_words, x_scales, wa, wb, gt, gi, off
         row = keep.tile([P, 2 * PACK * V], BF16, name="row", align_bytes=64)
         z2_planes = row[:, : PACK * V].rearrange("p (t v) -> p t v", t=PACK)
         z2_woven = row[:, PACK * V :].rearrange("p (v t) -> p v t", t=PACK)
-        for t in range(PACK - 1):
-            nc.scalar.activation(z2_planes[:, t, :], a_rows[t][:].indirect(fa_sb[:]), COPY)
 
-        last_plane = (PACK - 1) * V
+        def look_up(copy, t, first, last):
+            copy(z2_planes[:, t, first:last], a_rows[t][:].indirect(fa_sb[:, first // 16 : last // 16]))
+
+        def scalar_gather(dst, src):
+            nc.scalar.activation(dst, src, COPY)
+
+        for t, last in ((0, V), (1, V), (2, V // 2)):
+            look_up(scalar_gather, t, 0, last)
+
+        last_plane = 2 * V + V // 2
         wb_woven = [woven_tile("wb_woven0", HALF, "wa_pair1"), row[:, last_plane : last_plane + PACK * HALF].rearrange("p (c t) -> p c t", t=PACK)]
         wb_q = [operand("wb%d" % h, HALF) for h in range(2)]
         z_woven = [woven_tile("z_woven0", HALF, "wb_raw1"), woven_tile("z_woven1", HALF, "z_woven1")]
@@ -140,12 +147,14 @@ def tile_picked_gramsel_none_p_kernel(tc, x_words, x_scales, wa, wb, gt, gi, off
         def scale_chunk(c):
             nc.vector.tensor_tensor(z_woven[c // 2][:, chunk(c), :], project_chunk(c)[:].rearrange("p t n -> p n t"), gt_sb[:].unsqueeze(1).to_broadcast([P, CHUNK, PACK]), MULT)
 
-        weave(nc.vector.tensor_copy, wb_woven[0], wb_raw[0], 0, HALF)
-        quantise(nc, *wb_q[0], wb_woven[0], 0, HALF)
-        weave(nc.vector.tensor_copy, wb_woven[1], wb_raw[1], 0, HALF)
+        for h in range(2):
+            for u in range(2):
+                weave(nc.vector.tensor_copy, wb_woven[h], wb_raw[h], u * CHUNK, (u + 1) * CHUNK)
+            for u in range(2):
+                quantise(nc, *wb_q[h], wb_woven[h], u * CHUNK, (u + 1) * CHUNK)
         scale_chunk(0)
-        quantise(nc, *wb_q[1], wb_woven[1], 0, HALF)
-        nc.vector.tensor_copy(z2_planes[:, PACK - 1, :], a_rows[PACK - 1][:].indirect(fa_sb[:]))
+        look_up(nc.vector.tensor_copy, 2, V // 2, V)
+        look_up(nc.vector.tensor_copy, 3, 0, V)
         scale_chunk(1)
         weave(nc.vector.tensor_copy, z2_woven, z2_planes, 0, V)
         quantise(nc, *z_q[0], z_woven[0], 0, HALF)
@@ -176,6 +185,9 @@ def tile_picked_gramsel_none_p_kernel(tc, x_words, x_scales, wa, wb, gt, gi, off
             if len(banks) == 2:
                 for cols, bank, empty in ((slice(0, V // 2), banks[0], on_vector), (slice(V // 2, V), banks[1], on_scalar)):
                     empty(result[:, cols], product(c, cols, bank))
+                    if c == 2:
+                        (nc.sync if empty is on_vector else nc.scalar).dma_start(out[c * CHUNK : (c + 1) * CHUNK, cols], result[:, cols])
             else:
                 on_scalar(result[:], product(c, slice(0, V), banks[0]))
-            nc.sync.dma_start(out[c * CHUNK : (c + 1) * CHUNK, :], result[:])
+            if c != 2:
+                nc.sync.dma_start(out[c * CHUNK : (c + 1) * CHUNK, :], result[:])

@@ -113,7 +113,7 @@ def tile_picked_gramsel_none_p_kernel(tc, x_words, x_scales, wa, wb, gt, gi, off
         a_rows = [keep.tile([P, H], F32, name="a_rows%d" % t, tag="wa_pair0" if t == 0 else "a_rows%d" % t, align_bytes=64) for t in range(PACK)]
         for h in range(2):
             for t in range(PACK):
-                sums = psum.tile([P, HALF], F32, name="sums", tag="bank%d" % (0, 1, 4, 5)[t])
+                sums = psum.tile([P, HALF], F32, name="sums", tag="bank%d" % (PACK * h + t))
                 project(t, wa_q[h], whole, sums[:])
                 nc.scalar.activation(a_rows[t][:, h * HALF : (h + 1) * HALF], sums[:], COPY, scale=gi_sb[:, t : t + 1])
         row = keep.tile([P, 2 * PACK * V], BF16, name="row", align_bytes=64)
@@ -126,26 +126,26 @@ def tile_picked_gramsel_none_p_kernel(tc, x_words, x_scales, wa, wb, gt, gi, off
         def scalar_gather(dst, src):
             nc.scalar.activation(dst, src, COPY)
 
-        for t, last in ((0, V), (1, V), (2, V // 2)):
-            look_up(scalar_gather, t, 0, last)
+        for t in range(PACK - 1):
+            look_up(scalar_gather, t, 0, V)
 
-        last_plane = 2 * V + V // 2
+        last_plane = (PACK - 1) * V
         wb_woven = [woven_tile("wb_woven0", HALF, "wa_pair1"), row[:, last_plane : last_plane + PACK * HALF].rearrange("p (c t) -> p c t", t=PACK)]
         wb_q = [operand("wb%d" % h, HALF) for h in range(2)]
-        z_woven = [woven_tile("z_woven0", HALF, "wb_raw1"), woven_tile("z_woven1", HALF, "z_woven1")]
-        z_q = [operand("zhalf%d" % h, HALF) for h in range(2)]
+        z_woven = [woven_tile("z_woven0", CHUNK, "wb_raw1"), woven_tile("z_woven1", CHUNK, "a_rows3"), row[:, : PACK * CHUNK].rearrange("p (c t) -> p c t", t=PACK), woven_tile("z_woven3", CHUNK, "z_woven3")]
+        z_q = [operand("zchunk%d" % c, CHUNK) for c in range(H // CHUNK)]
 
         def chunk(c):
             return slice(c % 2 * CHUNK, (c % 2 + 1) * CHUNK)
 
         def project_chunk(c):
-            sums = psum.tile([P, PACK, CHUNK], F32, name="b_sums", tag="bank%d" % (2, 3, 6, 7)[c])
+            sums = psum.tile([P, PACK, CHUNK], F32, name="b_sums", tag="bank%d" % c)
             for t in range(PACK):
                 project(t, wb_q[c // 2], chunk(c), sums[:, t, :])
             return sums
 
         def scale_chunk(c):
-            nc.vector.tensor_tensor(z_woven[c // 2][:, chunk(c), :], project_chunk(c)[:].rearrange("p t n -> p n t"), gt_sb[:].unsqueeze(1).to_broadcast([P, CHUNK, PACK]), MULT)
+            nc.vector.tensor_tensor(z_woven[c][:, :, :], project_chunk(c)[:].rearrange("p t n -> p n t"), gt_sb[:].unsqueeze(1).to_broadcast([P, CHUNK, PACK]), MULT)
 
         for h in range(2):
             for u in range(2):
@@ -153,11 +153,11 @@ def tile_picked_gramsel_none_p_kernel(tc, x_words, x_scales, wa, wb, gt, gi, off
             for u in range(2):
                 quantise(nc, *wb_q[h], wb_woven[h], u * CHUNK, (u + 1) * CHUNK)
         scale_chunk(0)
-        look_up(nc.vector.tensor_copy, 2, V // 2, V)
         look_up(nc.vector.tensor_copy, 3, 0, V)
         scale_chunk(1)
+        quantise(nc, *z_q[0], z_woven[0], 0, CHUNK)
         weave(nc.vector.tensor_copy, z2_woven, z2_planes, 0, V)
-        quantise(nc, *z_q[0], z_woven[0], 0, HALF)
+        quantise(nc, *z_q[1], z_woven[1], 0, CHUNK)
         z2_q = operand("z2", V)
         quantise(nc, *z2_q, z2_woven, 0, V)
         scale_chunk(2)
@@ -165,13 +165,13 @@ def tile_picked_gramsel_none_p_kernel(tc, x_words, x_scales, wa, wb, gt, gi, off
         z_planes = keep.tile([P, PACK, CHUNK], BF16, name="z_planes", align_bytes=64)
         for t in range(PACK):
             nc.scalar.activation(z_planes[:, t, :], sums[:, t, :], COPY, scale=gt_sb[:, t : t + 1])
-        weave(nc.scalar.copy, z_woven[1][:, CHUNK:, :], z_planes, 0, CHUNK)
-        quantise(nc, *z_q[1], z_woven[1], CHUNK, HALF)
-        quantise(nc, *z_q[1], z_woven[1], 0, CHUNK)
+        weave(nc.scalar.copy, z_woven[3], z_planes, 0, CHUNK)
+        for c in (3, 2):
+            quantise(nc, *z_q[c], z_woven[c], 0, CHUNK)
 
         def product(c, cols, bank):
             sums = psum.tile([P, cols.stop - cols.start], F32, name="out_sums", tag="bank%d" % bank)
-            multiply(sums[:], z_q[c // 2], chunk(c), z2_q, cols)
+            multiply(sums[:], z_q[c], slice(0, CHUNK), z2_q, cols)
             return sums
 
         def on_vector(dst, sums):
@@ -180,7 +180,7 @@ def tile_picked_gramsel_none_p_kernel(tc, x_words, x_scales, wa, wb, gt, gi, off
         def on_scalar(dst, sums):
             nc.scalar.activation(dst, sums[:], COPY, scale=0.0625)
 
-        for c, banks in ((0, (4,)), (1, (5,)), (3, (0, 1)), (2, (2, 3))):
+        for c, banks in ((0, (4,)), (1, (5,)), (3, (6, 7)), (2, (0, 1))):
             result = keep.tile([P, V], F32, name="result%d" % c, align_bytes=64)
             if len(banks) == 2:
                 for cols, bank, empty in ((slice(0, V // 2), banks[0], on_vector), (slice(V // 2, V), banks[1], on_scalar)):

@@ -14,6 +14,7 @@ U8 = mybir.dt.uint8
 FP8X4 = mybir.dt.float8_e4m3fn_x4
 COPY = mybir.ActivationFunctionType.Copy
 MULT = mybir.AluOpType.mult
+ADD = mybir.AluOpType.add
 
 P = 128
 PACK = 4
@@ -35,6 +36,7 @@ def tile_picked_gramsel_none_p_kernel(tc, x_words, x_scales, wa, wb, gt, gi, off
     with ExitStack() as ctx:
         lists = ctx.enter_context(tc.tile_pool(name="lists", bufs=1))
         keep = ctx.enter_context(tc.tile_pool(name="keep", bufs=1))
+        shared = ctx.enter_context(tc.tile_pool(name="shared", bufs=1))
         psum = ctx.enter_context(tc.psum_pool(name="psum", bufs=1))
 
         def operand(name, width, tag=None):
@@ -44,6 +46,9 @@ def tile_picked_gramsel_none_p_kernel(tc, x_words, x_scales, wa, wb, gt, gi, off
 
         def woven_tile(name, width, tag):
             return keep.tile([P, width, PACK], BF16, name=name, tag=tag, align_bytes=64)
+
+        def laid(name, shape, dtype, offset):
+            return shared.tile(shape, dtype, name=name, offset=offset, align_bytes=64)
 
         offs_sb = lists.tile([P, S // 16], U16, name="offs_sb")
         fa_sb = lists.tile([P, V // 16], U16, name="fa_sb")
@@ -61,7 +66,7 @@ def tile_picked_gramsel_none_p_kernel(tc, x_words, x_scales, wa, wb, gt, gi, off
             return raw
 
         def load_pairs(w, h, name):
-            pairs = [keep.tile([P, 2, HALF], F32, name="%s%d" % (name, u), tag="%s%d" % (name, u), align_bytes=64) for u in range(2)]
+            pairs = [laid(name + "0", [P, 2, HALF], F32, 0), keep.tile([P, 2, HALF], F32, name=name + "1", align_bytes=64)]
             for u in range(2):
                 nc.sync.dma_start(pairs[u][:], half_rows(w, h)[:, 2 * u : 2 * u + 2, :])
             return pairs
@@ -110,62 +115,63 @@ def tile_picked_gramsel_none_p_kernel(tc, x_words, x_scales, wa, wb, gt, gi, off
             quantise(nc, *wa_q[1], wa_woven1, u * CHUNK, (u + 1) * CHUNK)
 
         whole = slice(0, HALF)
-        a_rows = [keep.tile([P, H], F32, name="a_rows%d" % t, tag="wa_pair0" if t == 0 else "a_rows%d" % t, align_bytes=64) for t in range(PACK)]
+        a_rows = [laid("a_rows0", [P, H], F32, 0)]
+        a_rows.extend(keep.tile([P, H], F32, name="a_rows%d" % t, tag="a_rows%d" % t, align_bytes=64) for t in range(1, PACK))
         for h in range(2):
             for t in range(PACK):
                 sums = psum.tile([P, HALF], F32, name="sums", tag="bank%d" % (PACK * h + t))
                 project(t, wa_q[h], whole, sums[:])
                 nc.scalar.activation(a_rows[t][:, h * HALF : (h + 1) * HALF], sums[:], COPY, scale=gi_sb[:, t : t + 1])
-        row = keep.tile([P, 2 * PACK * V], BF16, name="row", align_bytes=64)
-        z2_planes = row[:, : PACK * V].rearrange("p (t v) -> p t v", t=PACK)
-        z2_woven = row[:, PACK * V :].rearrange("p (v t) -> p v t", t=PACK)
 
-        def look_up(copy, t, first, last):
-            copy(z2_planes[:, t, first:last], a_rows[t][:].indirect(fa_sb[:, first // 16 : last // 16]))
+        wb_woven0 = laid("wb_woven0", [P, HALF, PACK], BF16, 5376)
+        wb_q = {c: operand("wb%d" % c, CHUNK) for c in range(2)}
+        for u in range(2):
+            weave(nc.vector.tensor_copy, wb_woven0, wb_raw[0], u * CHUNK, (u + 1) * CHUNK)
+        for u in range(2):
+            quantise(nc, *wb_q[u], wb_woven0[:, u * CHUNK : (u + 1) * CHUNK, :], 0, CHUNK)
+        wb_woven3 = laid("wb_woven3", [P, CHUNK, PACK], BF16, 2048)
+        weave(nc.vector.tensor_copy, wb_woven3, wb_raw[1][:, :, CHUNK:], 0, CHUNK)
 
-        def scalar_gather(dst, src):
-            nc.scalar.activation(dst, src, COPY)
+        z2_planes = laid("z2_planes", [P, PACK, V], BF16, 4352)
+        nc.vector.tensor_copy(z2_planes[:, 0, :], a_rows[0][:].indirect(fa_sb[:]))
+        for t in range(1, PACK):
+            nc.scalar.activation(z2_planes[:, t, :], a_rows[t][:].indirect(fa_sb[:]), COPY)
+        wb_q[3] = operand("wb3", CHUNK)
+        quantise(nc, *wb_q[3], wb_woven3, 0, CHUNK)
 
-        for t in range(PACK - 1):
-            look_up(scalar_gather, t, 0, V)
+        wb_woven2 = laid("wb_woven2", [P, CHUNK, PACK], BF16, 1536)
+        nc.gpsimd.tensor_scalar(wb_woven2[:], wb_raw[1][:, :, :CHUNK].rearrange("p t c -> p c t"), 1.0, 0.0, MULT, ADD)
 
-        last_plane = (PACK - 1) * V
-        wb_woven = [woven_tile("wb_woven0", HALF, "wa_pair1"), row[:, last_plane : last_plane + PACK * HALF].rearrange("p (c t) -> p c t", t=PACK)]
-        wb_q = [operand("wb%d" % h, HALF) for h in range(2)]
-        z_woven = [woven_tile("z_woven0", CHUNK, "wb_raw1"), woven_tile("z_woven1", CHUNK, "a_rows3"), row[:, : PACK * CHUNK].rearrange("p (c t) -> p c t", t=PACK), woven_tile("z_woven3", CHUNK, "z_woven3")]
-        z_q = [operand("zchunk%d" % c, CHUNK) for c in range(H // CHUNK)]
-
-        def chunk(c):
-            return slice(c % 2 * CHUNK, (c % 2 + 1) * CHUNK)
+        z_woven = [laid("z_woven0", [P, CHUNK, PACK], BF16, 0), woven_tile("z_woven1", CHUNK, "z_woven1"), laid("z_woven2", [P, CHUNK, PACK], BF16, 4352), woven_tile("z_woven3", CHUNK, "z_woven3")]
+        z_q = [(keep.tile([P, CHUNK], U32, name="zchunk%d_codes" % c, align_bytes=64), keep.tile([P, CHUNK], U8, name="zchunk%d_scales" % c, tag=("wb_raw1", "a_rows3")[c], align_bytes=64)) for c in range(2)]
+        z_q.append(operand("zchunk2", CHUNK))
 
         def project_chunk(c):
             sums = psum.tile([P, PACK, CHUNK], F32, name="b_sums", tag="bank%d" % c)
             for t in range(PACK):
-                project(t, wb_q[c // 2], chunk(c), sums[:, t, :])
+                project(t, wb_q[c], slice(0, CHUNK), sums[:, t, :])
             return sums
 
         def scale_chunk(c):
-            nc.vector.tensor_tensor(z_woven[c][:, :, :], project_chunk(c)[:].rearrange("p t n -> p n t"), gt_sb[:].unsqueeze(1).to_broadcast([P, CHUNK, PACK]), MULT)
+            nc.vector.tensor_tensor(z_woven[c][:], project_chunk(c)[:].rearrange("p t n -> p n t"), gt_sb[:].unsqueeze(1).to_broadcast([P, CHUNK, PACK]), MULT)
 
-        for h in range(2):
-            for u in range(2):
-                weave(nc.vector.tensor_copy, wb_woven[h], wb_raw[h], u * CHUNK, (u + 1) * CHUNK)
-            for u in range(2):
-                quantise(nc, *wb_q[h], wb_woven[h], u * CHUNK, (u + 1) * CHUNK)
         scale_chunk(0)
-        look_up(nc.vector.tensor_copy, 3, 0, V)
         scale_chunk(1)
+        sums = project_chunk(3)
+        wb_q[2] = operand("wb2", CHUNK, tag="wb1_codes")
+        quantise(nc, *wb_q[2], wb_woven2, 0, CHUNK)
         quantise(nc, *z_q[0], z_woven[0], 0, CHUNK)
+        z2_woven = laid("z2_woven", [P, V, PACK], BF16, 2304)
         weave(nc.vector.tensor_copy, z2_woven, z2_planes, 0, V)
         quantise(nc, *z_q[1], z_woven[1], 0, CHUNK)
         z2_q = operand("z2", V)
         quantise(nc, *z2_q, z2_woven, 0, V)
         scale_chunk(2)
-        sums = project_chunk(3)
-        z_planes = keep.tile([P, PACK, CHUNK], BF16, name="z_planes", align_bytes=64)
+        z_planes = keep.tile([P, PACK, CHUNK], BF16, name="z_planes", tag="a_rows2", align_bytes=64)
         for t in range(PACK):
             nc.scalar.activation(z_planes[:, t, :], sums[:, t, :], COPY, scale=gt_sb[:, t : t + 1])
         weave(nc.scalar.copy, z_woven[3], z_planes, 0, CHUNK)
+        z_q.append((keep.tile([P, CHUNK], U32, name="zchunk3_codes", align_bytes=64), laid("zchunk3_scales", [P, CHUNK], U8, 5376)))
         for c in (3, 2):
             quantise(nc, *z_q[c], z_woven[c], 0, CHUNK)
 

@@ -14,13 +14,13 @@ U8 = mybir.dt.uint8
 FP8X4 = mybir.dt.float8_e4m3fn_x4
 COPY = mybir.ActivationFunctionType.Copy
 MULT = mybir.AluOpType.mult
-ADD = mybir.AluOpType.add
 
 P = 128
 PACK = 4
 HALF = 256
 CHUNK = 128
 WA0_VECTOR = 64
+Z2_SCALAR = 64
 
 
 def weave(copy, dst, src, c0, c1):
@@ -123,27 +123,25 @@ def tile_picked_gramsel_none_p_kernel(tc, x_words, x_scales, wa, wb, gt, gi, off
                 project(t, wa_q[h], whole, sums[:])
                 nc.scalar.activation(a_rows[t][:, h * HALF : (h + 1) * HALF], sums[:], COPY, scale=gi_sb[:, t : t + 1])
 
-        wb_woven0 = laid("wb_woven0", [P, HALF, PACK], BF16, 5376)
-        wb_q = {c: operand("wb%d" % c, CHUNK) for c in range(2)}
-        for u in range(2):
-            weave(nc.vector.tensor_copy, wb_woven0, wb_raw[0], u * CHUNK, (u + 1) * CHUNK)
-        for u in range(2):
-            quantise(nc, *wb_q[u], wb_woven0[:, u * CHUNK : (u + 1) * CHUNK, :], 0, CHUNK)
-        wb_woven3 = laid("wb_woven3", [P, CHUNK, PACK], BF16, 2048)
-        weave(nc.vector.tensor_copy, wb_woven3, wb_raw[1][:, :, CHUNK:], 0, CHUNK)
+        wb_woven = [laid("wb_woven0", [P, HALF, PACK], BF16, 6144), laid("wb_woven1", [P, HALF, PACK], BF16, 2048)]
+        wb_q = [operand("wb%d" % c, CHUNK) for c in range(H // CHUNK)]
+
+        def quantise_wb(c):
+            quantise(nc, *wb_q[c], wb_woven[c // 2][:, c % 2 * CHUNK : (c % 2 + 1) * CHUNK, :], 0, CHUNK)
+
+        for h in range(2):
+            for u in range(2):
+                weave(nc.vector.tensor_copy, wb_woven[h], wb_raw[h], u * CHUNK, (u + 1) * CHUNK)
+            for u in range(2):
+                quantise_wb(2 * h + u)
 
         z2_planes = laid("z2_planes", [P, PACK, V], BF16, 4352)
         nc.vector.tensor_copy(z2_planes[:, 0, :], a_rows[0][:].indirect(fa_sb[:]))
         for t in range(1, PACK):
             nc.scalar.activation(z2_planes[:, t, :], a_rows[t][:].indirect(fa_sb[:]), COPY)
-        wb_q[3] = operand("wb3", CHUNK)
-        quantise(nc, *wb_q[3], wb_woven3, 0, CHUNK)
 
-        wb_woven2 = laid("wb_woven2", [P, CHUNK, PACK], BF16, 1536)
-        nc.gpsimd.tensor_scalar(wb_woven2[:], wb_raw[1][:, :, :CHUNK].rearrange("p t c -> p c t"), 1.0, 0.0, MULT, ADD)
-
-        z_woven = [laid("z_woven0", [P, CHUNK, PACK], BF16, 0), woven_tile("z_woven1", CHUNK, "z_woven1"), laid("z_woven2", [P, CHUNK, PACK], BF16, 4352), woven_tile("z_woven3", CHUNK, "z_woven3")]
-        z_q = [(keep.tile([P, CHUNK], U32, name="zchunk%d_codes" % c, align_bytes=64), keep.tile([P, CHUNK], U8, name="zchunk%d_scales" % c, tag=("wb_raw1", "a_rows3")[c], align_bytes=64)) for c in range(2)]
+        z_woven = [woven_tile("z_woven0", CHUNK, "wb_raw1"), laid("z_woven1", [P, CHUNK, PACK], BF16, 0), laid("z_woven2", [P, CHUNK, PACK], BF16, 4352), woven_tile("z_woven3", CHUNK, "z_woven3")]
+        z_q = [(keep.tile([P, CHUNK], U32, name="zchunk%d_codes" % c, align_bytes=64), keep.tile([P, CHUNK], U8, name="zchunk%d_scales" % c, tag=("wb1_codes", "a_rows3")[c], align_bytes=64)) for c in range(2)]
         z_q.append(operand("zchunk2", CHUNK))
 
         def project_chunk(c):
@@ -157,16 +155,15 @@ def tile_picked_gramsel_none_p_kernel(tc, x_words, x_scales, wa, wb, gt, gi, off
 
         scale_chunk(0)
         scale_chunk(1)
-        sums = project_chunk(3)
-        wb_q[2] = operand("wb2", CHUNK, tag="wb1_codes")
-        quantise(nc, *wb_q[2], wb_woven2, 0, CHUNK)
         quantise(nc, *z_q[0], z_woven[0], 0, CHUNK)
         z2_woven = laid("z2_woven", [P, V, PACK], BF16, 2304)
-        weave(nc.vector.tensor_copy, z2_woven, z2_planes, 0, V)
+        weave(nc.vector.tensor_copy, z2_woven, z2_planes, Z2_SCALAR, V)
+        weave(nc.scalar.copy, z2_woven, z2_planes, 0, Z2_SCALAR)
         quantise(nc, *z_q[1], z_woven[1], 0, CHUNK)
         z2_q = operand("z2", V)
         quantise(nc, *z2_q, z2_woven, 0, V)
         scale_chunk(2)
+        sums = project_chunk(3)
         z_planes = keep.tile([P, PACK, CHUNK], BF16, name="z_planes", tag="a_rows2", align_bytes=64)
         for t in range(PACK):
             nc.scalar.activation(z_planes[:, t, :], sums[:, t, :], COPY, scale=gt_sb[:, t : t + 1])

@@ -129,10 +129,10 @@ def tile_picked_gramsel_none_p_kernel(tc, x_words, x_scales, wa, wb, gt, gi, off
         def quantise_wb(c):
             quantise(nc, *wb_q[c], wb_woven[c // 2][:, c % 2 * CHUNK : (c % 2 + 1) * CHUNK, :], 0, CHUNK)
 
-        for h in range(2):
-            for u in range(2):
+        for h, order in enumerate(((0, 1), (1, 0))):
+            for u in order:
                 weave(nc.vector.tensor_copy, wb_woven[h], wb_raw[h], u * CHUNK, (u + 1) * CHUNK)
-            for u in range(2):
+            for u in order:
                 quantise_wb(2 * h + u)
 
         z2_planes = laid("z2_planes", [P, PACK, V], BF16, 4352)
@@ -184,13 +184,13 @@ def tile_picked_gramsel_none_p_kernel(tc, x_words, x_scales, wa, wb, gt, gi, off
             nc.scalar.activation(dst, sums[:], COPY, scale=0.0625)
 
         for c, banks in ((0, (4,)), (1, (5,)), (3, (6, 7)), (2, (0, 1))):
-            result = keep.tile([P, V], F32, name="result%d" % c, align_bytes=64)
+            result = keep.tile([P, V], F32, name="result%d" % c, tag="z_woven3" if c == 1 else "result%d" % c, align_bytes=64)
             if len(banks) == 2:
                 for cols, bank, empty in ((slice(0, V // 2), banks[0], on_vector), (slice(V // 2, V), banks[1], on_scalar)):
                     empty(result[:, cols], product(c, cols, bank))
                     if c == 2:
                         (nc.sync if empty is on_vector else nc.scalar).dma_start(out[c * CHUNK : (c + 1) * CHUNK, cols], result[:, cols])
             else:
-                on_scalar(result[:], product(c, slice(0, V), banks[0]))
+                (on_vector if c else on_scalar)(result[:], product(c, slice(0, V), banks[0]))
             if c != 2:
                 nc.sync.dma_start(out[c * CHUNK : (c + 1) * CHUNK, :], result[:])

@@ -53,7 +53,7 @@ def tile_picked_gramsel_none_p_kernel(tc, x_words, x_scales, wa, wb, gt, gi, off
         offs_sb = lists.tile([P, S // 16], U16, name="offs_sb")
         fa_sb = lists.tile([P, V // 16], U16, name="fa_sb")
         xw = keep.tile([P, T], U32, name="xw", align_bytes=64)
-        xs = keep.tile([P, T], U8, name="xs", align_bytes=64)
+        xs = keep.tile([P, T], U8, name="xs", tag="xs", align_bytes=64)
         gt_sb = keep.tile([P, PACK], F32, name="gt_sb", align_bytes=64)
         gi_sb = keep.tile([P, PACK], F32, name="gi_sb", align_bytes=64)
 
@@ -72,8 +72,8 @@ def tile_picked_gramsel_none_p_kernel(tc, x_words, x_scales, wa, wb, gt, gi, off
             return pairs
 
         nc.vector.memset(xs[:].bitcast(I32), 0)
-        nc.sync.dma_start(offs_sb[:], offs)
         wa_raw0 = load_half(wa, 0, "wa_raw0")
+        nc.sync.dma_start(offs_sb[:], offs)
         for q in range(4):
             nc.sync.dma_start(xs[32 * q : 32 * q + 4, :].bitcast(I32), x_scales[0, 4 * q : 4 * q + 4, :].bitcast(I32))
         nc.sync.dma_start(xw[:].bitcast(I32), x_words[0].rearrange("p n t -> p (n t)").bitcast(I32))
@@ -88,7 +88,7 @@ def tile_picked_gramsel_none_p_kernel(tc, x_words, x_scales, wa, wb, gt, gi, off
         weave(nc.scalar.copy, wa_woven0, wa_raw0, WA0_VECTOR, HALF)
         xq_scales = keep.tile([P, S], U8, name="xq_scales", align_bytes=64)
         nc.vector.tensor_copy(xq_scales[:].rearrange("p (t m) -> p m t", t=PACK), xs[:].indirect(offs_sb[:]))
-        wa_q = [operand("wa%d" % h, HALF) for h in range(2)]
+        wa_q = [operand("wa0", HALF, tag="xs"), operand("wa1", HALF)]
         quantise(nc, *wa_q[0], wa_woven0, 0, HALF)
         xq_codes = keep.tile([P, S], U32, name="xq_codes", tag="wa_woven0", align_bytes=64)
         nc.vector.tensor_copy(xq_codes[:].rearrange("p (t m) -> p m t", t=PACK), xw[:].indirect(offs_sb[:]))
@@ -189,7 +189,7 @@ def tile_picked_gramsel_none_p_kernel(tc, x_words, x_scales, wa, wb, gt, gi, off
                 for cols, bank, empty in ((slice(0, V // 2), banks[0], on_vector), (slice(V // 2, V), banks[1], on_scalar)):
                     empty(result[:, cols], product(c, cols, bank))
                     if c == 2:
-                        (nc.sync if empty is on_vector else nc.scalar).dma_start(out[c * CHUNK : (c + 1) * CHUNK, cols], result[:, cols])
+                        nc.sync.dma_start(out[c * CHUNK : (c + 1) * CHUNK, cols], result[:, cols])
             else:
                 (on_vector if c else on_scalar)(result[:], product(c, slice(0, V), banks[0]))
             if c != 2:

@@ -19,7 +19,7 @@ P = 128
 PACK = 4
 HALF = 256
 CHUNK = 128
-WA0_VECTOR = 64
+WA0_VECTOR = 128
 Z2_SCALAR = 64
 
 
@@ -86,11 +86,11 @@ def tile_picked_gramsel_none_p_kernel(tc, x_words, x_scales, wa, wb, gt, gi, off
         wa_woven0 = woven_tile("wa_woven0", HALF, "wa_woven0")
         weave(nc.vector.tensor_copy, wa_woven0, wa_raw0, 0, WA0_VECTOR)
         weave(nc.scalar.copy, wa_woven0, wa_raw0, WA0_VECTOR, HALF)
-        xq_scales = keep.tile([P, S], U8, name="xq_scales", align_bytes=64)
-        nc.vector.tensor_copy(xq_scales[:].rearrange("p (t m) -> p m t", t=PACK), xs[:].indirect(offs_sb[:]))
-        wa_q = [operand("wa0", HALF, tag="xs"), operand("wa1", HALF)]
+        wa_q = [operand("wa0", HALF), operand("wa1", HALF)]
         quantise(nc, *wa_q[0], wa_woven0, 0, HALF)
-        xq_codes = keep.tile([P, S], U32, name="xq_codes", tag="wa_woven0", align_bytes=64)
+        xq_scales = keep.tile([P, S], U8, name="xq_scales", tag="wa_woven0", align_bytes=64)
+        nc.vector.tensor_copy(xq_scales[:].rearrange("p (t m) -> p m t", t=PACK), xs[:].indirect(offs_sb[:]))
+        xq_codes = keep.tile([P, S], U32, name="xq_codes", align_bytes=64)
         nc.vector.tensor_copy(xq_codes[:].rearrange("p (t m) -> p m t", t=PACK), xw[:].indirect(offs_sb[:]))
 
         def multiply(sums, stationary, rows, moving, cols):

@@ -132,11 +132,12 @@ def tile_picked_gramsel_none_p_kernel(tc, x_words, x_scales, wa, wb, gt, gi, off
         for h, order in enumerate(((0, 1), (1, 0))):
             for u in order:
                 weave(nc.vector.tensor_copy, wb_woven[h], wb_raw[h], u * CHUNK, (u + 1) * CHUNK)
-            for u in order:
+            for u in order[: 2 - h]:
                 quantise_wb(2 * h + u)
 
         z2_planes = laid("z2_planes", [P, PACK, V], BF16, 4352)
         nc.vector.tensor_copy(z2_planes[:, 0, :], a_rows[0][:].indirect(fa_sb[:]))
+        quantise_wb(2)
         for t in range(1, PACK):
             nc.scalar.activation(z2_planes[:, t, :], a_rows[t][:].indirect(fa_sb[:]), COPY)
 
@@ -184,13 +185,13 @@ def tile_picked_gramsel_none_p_kernel(tc, x_words, x_scales, wa, wb, gt, gi, off
             nc.scalar.activation(dst, sums[:], COPY, scale=0.0625)
 
         for c, banks in ((0, (4,)), (1, (5,)), (3, (6, 7)), (2, (0, 1))):
-            result = keep.tile([P, V], F32, name="result%d" % c, tag="z_woven3" if c == 1 else "result%d" % c, align_bytes=64)
+            result = keep.tile([P, V], F32, name="result%d" % c, tag="result%d" % c, align_bytes=64)
             if len(banks) == 2:
                 for cols, bank, empty in ((slice(0, V // 2), banks[0], on_vector), (slice(V // 2, V), banks[1], on_scalar)):
                     empty(result[:, cols], product(c, cols, bank))
                     if c == 2:
                         nc.sync.dma_start(out[c * CHUNK : (c + 1) * CHUNK, cols], result[:, cols])
             else:
-                (on_vector if c else on_scalar)(result[:], product(c, slice(0, V), banks[0]))
+                on_scalar(result[:], product(c, slice(0, V), banks[0]))
             if c != 2:
                 nc.sync.dma_start(out[c * CHUNK : (c + 1) * CHUNK, :], result[:])

@@ -20,6 +20,7 @@ PACK = 4
 HALF = 256
 CHUNK = 128
 WA0_VECTOR = 128
+WA1_SCALAR = 80
 Z2_SCALAR = 64
 
 
@@ -65,19 +66,13 @@ def tile_picked_gramsel_none_p_kernel(tc, x_words, x_scales, wa, wb, gt, gi, off
             nc.sync.dma_start(raw[:], half_rows(w, h))
             return raw
 
-        def load_pairs(w, h, name):
-            pairs = [laid(name + "0", [P, 2, HALF], F32, 0), keep.tile([P, 2, HALF], F32, name=name + "1", align_bytes=64)]
-            for u in range(2):
-                nc.sync.dma_start(pairs[u][:], half_rows(w, h)[:, 2 * u : 2 * u + 2, :])
-            return pairs
-
         nc.vector.memset(xs[:].bitcast(I32), 0)
         wa_raw0 = load_half(wa, 0, "wa_raw0")
         nc.sync.dma_start(offs_sb[:], offs)
         for q in range(4):
             nc.sync.dma_start(xs[32 * q : 32 * q + 4, :].bitcast(I32), x_scales[0, 4 * q : 4 * q + 4, :].bitcast(I32))
         nc.sync.dma_start(xw[:].bitcast(I32), x_words[0].rearrange("p n t -> p (n t)").bitcast(I32))
-        wa_raw1 = load_pairs(wa, 1, "wa_pair")
+        wa_raw1 = load_half(wa, 1, "wa_raw1")
         nc.sync.dma_start(gi_sb[:], gi.rearrange("(p t) o -> p (t o)", t=PACK))
         wb_raw = [load_half(wb, h, "wb_raw%d" % h) for h in range(2)]
         nc.sync.dma_start(fa_sb[:], fa)
@@ -108,10 +103,10 @@ def tile_picked_gramsel_none_p_kernel(tc, x_words, x_scales, wa, wb, gt, gi, off
             multiply(sums, (xq_codes, xq_scales), slice(t * P, (t + 1) * P), weights, cols)
 
         wa_woven1 = woven_tile("wa_woven1", HALF, "wa_woven1")
-        weave(nc.scalar.copy, wa_woven1[:, :, :2], wa_raw1[0], 0, HALF)
-        for u in range(2):
-            weave(nc.vector.tensor_copy, wa_woven1[:, :, 2:], wa_raw1[1], u * CHUNK, (u + 1) * CHUNK)
-        for u in range(2):
+        weave(nc.scalar.copy, wa_woven1, wa_raw1, 0, WA1_SCALAR)
+        weave(nc.vector.tensor_copy, wa_woven1, wa_raw1, CHUNK, HALF)
+        weave(nc.vector.tensor_copy, wa_woven1, wa_raw1, WA1_SCALAR, CHUNK)
+        for u in (1, 0):
             quantise(nc, *wa_q[1], wa_woven1, u * CHUNK, (u + 1) * CHUNK)
 
         whole = slice(0, HALF)

@@ -124,7 +124,7 @@ def tile_picked_gramsel_none_p_kernel(tc, x_words, x_scales, wa, wb, gt, gi, off
         def quantise_wb(c):
             quantise(nc, *wb_q[c], wb_woven[c // 2][:, c % 2 * CHUNK : (c % 2 + 1) * CHUNK, :], 0, CHUNK)
 
-        for h, order in enumerate(((0, 1), (1, 0))):
+        for h, order in enumerate(((0, 1), (0, 1))):
             for u in order:
                 weave(nc.vector.tensor_copy, wb_woven[h], wb_raw[h], u * CHUNK, (u + 1) * CHUNK)
             for u in order[: 2 - h]:
@@ -132,7 +132,7 @@ def tile_picked_gramsel_none_p_kernel(tc, x_words, x_scales, wa, wb, gt, gi, off
 
         z2_planes = laid("z2_planes", [P, PACK, V], BF16, 4352)
         nc.vector.tensor_copy(z2_planes[:, 0, :], a_rows[0][:].indirect(fa_sb[:]))
-        quantise_wb(2)
+        quantise_wb(3)
         for t in range(1, PACK):
             nc.scalar.activation(z2_planes[:, t, :], a_rows[t][:].indirect(fa_sb[:]), COPY)
 
@@ -141,7 +141,7 @@ def tile_picked_gramsel_none_p_kernel(tc, x_words, x_scales, wa, wb, gt, gi, off
         z_q.append(operand("zchunk2", CHUNK))
 
         def project_chunk(c):
-            sums = psum.tile([P, PACK, CHUNK], F32, name="b_sums", tag="bank%d" % c)
+            sums = psum.tile([P, PACK, CHUNK], F32, name="b_sums", tag="bank%d" % (0, 1, 1, 3)[c])
             for t in range(PACK):
                 project(t, wb_q[c], slice(0, CHUNK), sums[:, t, :])
             return sums

@@ -21,7 +21,6 @@ HALF = 256
 CHUNK = 128
 WA0_VECTOR = 128
 WA1_SCALAR = 80
-Z2_SCALAR = 64
 
 
 def weave(copy, dst, src, c0, c1):
@@ -40,30 +39,25 @@ def tile_picked_gramsel_none_p_kernel(tc, x_words, x_scales, wa, wb, gt, gi, off
         shared = ctx.enter_context(tc.tile_pool(name="shared", bufs=1))
         psum = ctx.enter_context(tc.psum_pool(name="psum", bufs=1))
 
-        def operand(name, width, tag=None):
-            codes = keep.tile([P, width], U32, name=name + "_codes", tag=tag or name + "_codes", align_bytes=64)
-            scales = keep.tile([P, width], U8, name=name + "_scales", align_bytes=64)
-            return codes, scales
-
-        def woven_tile(name, width, tag):
-            return keep.tile([P, width, PACK], BF16, name=name, tag=tag, align_bytes=64)
+        def held(name, shape, dtype, tag=None):
+            return keep.tile(shape, dtype, name=name, tag=tag or name, align_bytes=64)
 
         def laid(name, shape, dtype, offset):
             return shared.tile(shape, dtype, name=name, offset=offset, align_bytes=64)
 
+        def operand(name, width, codes_tag=None, scales_tag=None):
+            return held(name + "_codes", [P, width], U32, codes_tag), held(name + "_scales", [P, width], U8, scales_tag)
+
         offs_sb = lists.tile([P, S // 16], U16, name="offs_sb")
         fa_sb = lists.tile([P, V // 16], U16, name="fa_sb")
-        xw = keep.tile([P, T], U32, name="xw", align_bytes=64)
-        xs = keep.tile([P, T], U8, name="xs", tag="xs", align_bytes=64)
-        gt_sb = keep.tile([P, PACK], F32, name="gt_sb", align_bytes=64)
-        gi_sb = keep.tile([P, PACK], F32, name="gi_sb", align_bytes=64)
-
-        def half_rows(w, h):
-            return w[:, h * HALF : (h + 1) * HALF].rearrange("(p t) c -> p t c", t=PACK)
+        xw = held("xw", [P, T], U32)
+        xs = held("xs", [P, T], U8)
+        gt_sb = held("gt_sb", [P, PACK], F32)
+        gi_sb = held("gi_sb", [P, PACK], F32)
 
         def load_half(w, h, name):
-            raw = keep.tile([P, PACK, HALF], F32, name=name, tag=name, align_bytes=64)
-            nc.sync.dma_start(raw[:], half_rows(w, h))
+            raw = held(name, [P, PACK, HALF], F32)
+            nc.sync.dma_start(raw[:], w[:, h * HALF : (h + 1) * HALF].rearrange("(p t) c -> p t c", t=PACK))
             return raw
 
         nc.vector.memset(xs[:].bitcast(I32), 0)
@@ -74,18 +68,19 @@ def tile_picked_gramsel_none_p_kernel(tc, x_words, x_scales, wa, wb, gt, gi, off
         nc.sync.dma_start(xw[:].bitcast(I32), x_words[0].rearrange("p n t -> p (n t)").bitcast(I32))
         wa_raw1 = load_half(wa, 1, "wa_raw1")
         nc.sync.dma_start(gi_sb[:], gi.rearrange("(p t) o -> p (t o)", t=PACK))
-        wb_raw = [load_half(wb, h, "wb_raw%d" % h) for h in range(2)]
         nc.sync.dma_start(fa_sb[:], fa)
+        wb_raw0 = load_half(wb, 0, "wb_raw0")
+        wb_raw1 = load_half(wb, 1, "wb_raw1")
         nc.sync.dma_start(gt_sb[:], gt.rearrange("(p t) o -> p (t o)", t=PACK))
 
-        wa_woven0 = woven_tile("wa_woven0", HALF, "wa_woven0")
+        wa_woven0 = held("wa_woven0", [P, HALF, PACK], BF16)
         weave(nc.vector.tensor_copy, wa_woven0, wa_raw0, 0, WA0_VECTOR)
         weave(nc.scalar.copy, wa_woven0, wa_raw0, WA0_VECTOR, HALF)
         wa_q = [operand("wa0", HALF), operand("wa1", HALF)]
         quantise(nc, *wa_q[0], wa_woven0, 0, HALF)
-        xq_scales = keep.tile([P, S], U8, name="xq_scales", tag="wa_woven0", align_bytes=64)
+        xq_scales = held("xq_scales", [P, S], U8, "wa_woven0")
         nc.vector.tensor_copy(xq_scales[:].rearrange("p (t m) -> p m t", t=PACK), xs[:].indirect(offs_sb[:]))
-        xq_codes = keep.tile([P, S], U32, name="xq_codes", align_bytes=64)
+        xq_codes = held("xq_codes", [P, S], U32)
         nc.vector.tensor_copy(xq_codes[:].rearrange("p (t m) -> p m t", t=PACK), xw[:].indirect(offs_sb[:]))
 
         def multiply(sums, stationary, rows, moving, cols):
@@ -102,43 +97,53 @@ def tile_picked_gramsel_none_p_kernel(tc, x_words, x_scales, wa, wb, gt, gi, off
         def project(t, weights, cols, sums):
             multiply(sums, (xq_codes, xq_scales), slice(t * P, (t + 1) * P), weights, cols)
 
-        wa_woven1 = woven_tile("wa_woven1", HALF, "wa_woven1")
+        wa_woven1 = held("wa_woven1", [P, HALF, PACK], BF16)
         weave(nc.scalar.copy, wa_woven1, wa_raw1, 0, WA1_SCALAR)
         weave(nc.vector.tensor_copy, wa_woven1, wa_raw1, CHUNK, HALF)
         weave(nc.vector.tensor_copy, wa_woven1, wa_raw1, WA1_SCALAR, CHUNK)
         for u in (1, 0):
             quantise(nc, *wa_q[1], wa_woven1, u * CHUNK, (u + 1) * CHUNK)
 
-        whole = slice(0, HALF)
-        a_rows = [laid("a_rows0", [P, H], F32, 0)]
-        a_rows.extend(keep.tile([P, H], F32, name="a_rows%d" % t, tag="a_rows%d" % t, align_bytes=64) for t in range(1, PACK))
-        for h in range(2):
-            for t in range(PACK):
-                sums = psum.tile([P, HALF], F32, name="sums", tag="bank%d" % (PACK * h + t))
-                project(t, wa_q[h], whole, sums[:])
-                nc.scalar.activation(a_rows[t][:, h * HALF : (h + 1) * HALF], sums[:], COPY, scale=gi_sb[:, t : t + 1])
+        a_rows = [held("a_rows%d" % t, [P, H], F32) for t in range(PACK)]
+        z2_pairs = held("z2_pairs", [P, 2, V, 2], BF16)
 
-        wb_woven = [laid("wb_woven0", [P, HALF, PACK], BF16, 6144), laid("wb_woven1", [P, HALF, PACK], BF16, 2048)]
+        def look_up(t):
+            nc.scalar.activation(z2_pairs[:, t // 2, :, t % 2], a_rows[t][:].indirect(fa_sb[:]), COPY)
+
+        late = []
+        for h, t, bank in ((0, 0, 0), (0, 1, 1), (0, 2, 2), (1, 0, 4), (1, 1, 5), (1, 2, 6), (1, 3, 7), (0, 3, 4)):
+            sums = psum.tile([P, HALF], F32, name="sums", tag="bank%d" % bank)
+            project(t, wa_q[h], slice(0, HALF), sums[:])
+            dst = a_rows[t][:, h * HALF : (h + 1) * HALF]
+            if bank < 6:
+                nc.scalar.activation(dst, sums[:], COPY, scale=gi_sb[:, t : t + 1])
+            else:
+                late.append((dst, sums, t))
+            if (h, t) == (1, 1):
+                look_up(0)
+                look_up(1)
+
+        wb_woven1 = laid("wb_woven1", [P, HALF, PACK], BF16, 0)
+        wb_woven = [a_rows[2 + u][:, HALF:H].bitcast(BF16).rearrange("p (c t) -> p c t", t=PACK) for u in range(2)]
+        wb_woven.extend(wb_woven1[:, u * CHUNK : (u + 1) * CHUNK, :] for u in range(2))
         wb_q = [operand("wb%d" % c, CHUNK) for c in range(H // CHUNK)]
 
-        def quantise_wb(c):
-            quantise(nc, *wb_q[c], wb_woven[c // 2][:, c % 2 * CHUNK : (c % 2 + 1) * CHUNK, :], 0, CHUNK)
+        def prepare_wb(h, raw):
+            for u in range(2):
+                weave(nc.vector.tensor_copy, wb_woven[2 * h + u], raw[:, :, u * CHUNK : (u + 1) * CHUNK], 0, CHUNK)
+            for u in range(2):
+                quantise(nc, *wb_q[2 * h + u], wb_woven[2 * h + u], 0, CHUNK)
 
-        for h, order in enumerate(((0, 1), (0, 1))):
-            for u in order:
-                weave(nc.vector.tensor_copy, wb_woven[h], wb_raw[h], u * CHUNK, (u + 1) * CHUNK)
-            for u in order[: 2 - h]:
-                quantise_wb(2 * h + u)
+        prepare_wb(0, wb_raw0)
+        for dst, sums, t in late:
+            nc.vector.tensor_scalar(dst, sums[:], gi_sb[:, t : t + 1], None, MULT)
+        prepare_wb(1, wb_raw1)
 
-        z2_planes = laid("z2_planes", [P, PACK, V], BF16, 4352)
-        nc.vector.tensor_copy(z2_planes[:, 0, :], a_rows[0][:].indirect(fa_sb[:]))
-        quantise_wb(3)
-        for t in range(1, PACK):
-            nc.scalar.activation(z2_planes[:, t, :], a_rows[t][:].indirect(fa_sb[:]), COPY)
+        look_up(2)
+        look_up(3)
 
-        z_woven = [woven_tile("z_woven0", CHUNK, "wb_raw1"), laid("z_woven1", [P, CHUNK, PACK], BF16, 0), laid("z_woven2", [P, CHUNK, PACK], BF16, 4352), woven_tile("z_woven3", CHUNK, "z_woven3")]
-        z_q = [(keep.tile([P, CHUNK], U32, name="zchunk%d_codes" % c, align_bytes=64), keep.tile([P, CHUNK], U8, name="zchunk%d_scales" % c, tag=("wb1_codes", "a_rows3")[c], align_bytes=64)) for c in range(2)]
-        z_q.append(operand("zchunk2", CHUNK))
+        z_woven = [held("z_woven0", [P, CHUNK, PACK], BF16, "wb_raw1"), laid("z_woven1", [P, CHUNK, PACK], BF16, 0), held("z_woven2", [P, CHUNK, PACK], BF16, "z2_pairs"), held("z_woven3", [P, CHUNK, PACK], BF16)]
+        z_q = [operand("zchunk%d" % c, CHUNK) for c in range(3)]
 
         def project_chunk(c):
             sums = psum.tile([P, PACK, CHUNK], F32, name="b_sums", tag="bank%d" % (0, 1, 1, 3)[c])
@@ -152,19 +157,18 @@ def tile_picked_gramsel_none_p_kernel(tc, x_words, x_scales, wa, wb, gt, gi, off
         scale_chunk(0)
         scale_chunk(1)
         quantise(nc, *z_q[0], z_woven[0], 0, CHUNK)
-        z2_woven = laid("z2_woven", [P, V, PACK], BF16, 2304)
-        weave(nc.vector.tensor_copy, z2_woven, z2_planes, Z2_SCALAR, V)
-        weave(nc.scalar.copy, z2_woven, z2_planes, 0, Z2_SCALAR)
+        z2_woven = laid("z2_woven", [P, V, PACK], BF16, 1024)
+        nc.vector.tensor_copy(z2_woven[:].bitcast(I32), z2_pairs[:].rearrange("p u v e -> p u (v e)").bitcast(I32).rearrange("p u v -> p v u"))
         quantise(nc, *z_q[1], z_woven[1], 0, CHUNK)
         z2_q = operand("z2", V)
         quantise(nc, *z2_q, z2_woven, 0, V)
         scale_chunk(2)
         sums = project_chunk(3)
-        z_planes = keep.tile([P, PACK, CHUNK], BF16, name="z_planes", tag="a_rows2", align_bytes=64)
+        z_planes = held("z_planes", [P, PACK, CHUNK], BF16, "a_rows3")
         for t in range(PACK):
             nc.scalar.activation(z_planes[:, t, :], sums[:, t, :], COPY, scale=gt_sb[:, t : t + 1])
         weave(nc.scalar.copy, z_woven[3], z_planes, 0, CHUNK)
-        z_q.append((keep.tile([P, CHUNK], U32, name="zchunk3_codes", align_bytes=64), laid("zchunk3_scales", [P, CHUNK], U8, 5376)))
+        z_q.append((held("zchunk3_codes", [P, CHUNK], U32), laid("zchunk3_scales", [P, CHUNK], U8, 2048)))
         for c in (3, 2):
             quantise(nc, *z_q[c], z_woven[c], 0, CHUNK)
 
@@ -180,7 +184,7 @@ def tile_picked_gramsel_none_p_kernel(tc, x_words, x_scales, wa, wb, gt, gi, off
             nc.scalar.activation(dst, sums[:], COPY, scale=0.0625)
 
         for c, banks in ((0, (4,)), (1, (5,)), (3, (6, 7)), (2, (0, 1))):
-            result = keep.tile([P, V], F32, name="result%d" % c, tag="result%d" % c, align_bytes=64)
+            result = held("result%d" % c, [P, V], F32)
             if len(banks) == 2:
                 for cols, bank, empty in ((slice(0, V // 2), banks[0], on_vector), (slice(V // 2, V), banks[1], on_scalar)):
                     empty(result[:, cols], product(c, cols, bank))

@@ -128,16 +128,20 @@ def tile_picked_gramsel_none_p_kernel(tc, x_words, x_scales, wa, wb, gt, gi, off
         wb_woven.extend(wb_woven1[:, u * CHUNK : (u + 1) * CHUNK, :] for u in range(2))
         wb_q = [operand("wb%d" % c, CHUNK) for c in range(H // CHUNK)]
 
-        def prepare_wb(h, raw):
-            for u in range(2):
+        def weave_wb(h, raw):
+            for u in (h, 1 - h):
                 weave(nc.vector.tensor_copy, wb_woven[2 * h + u], raw[:, :, u * CHUNK : (u + 1) * CHUNK], 0, CHUNK)
-            for u in range(2):
-                quantise(nc, *wb_q[2 * h + u], wb_woven[2 * h + u], 0, CHUNK)
 
-        prepare_wb(0, wb_raw0)
+        def quantise_wb(c):
+            quantise(nc, *wb_q[c], wb_woven[c], 0, CHUNK)
+
+        weave_wb(0, wb_raw0)
+        quantise_wb(0)
+        quantise_wb(1)
         for dst, sums, t in late:
             nc.vector.tensor_scalar(dst, sums[:], gi_sb[:, t : t + 1], None, MULT)
-        prepare_wb(1, wb_raw1)
+        weave_wb(1, wb_raw1)
+        quantise_wb(3)
 
         look_up(2)
         look_up(3)
@@ -146,7 +150,7 @@ def tile_picked_gramsel_none_p_kernel(tc, x_words, x_scales, wa, wb, gt, gi, off
         z_q = [operand("zchunk%d" % c, CHUNK) for c in range(3)]
 
         def project_chunk(c):
-            sums = psum.tile([P, PACK, CHUNK], F32, name="b_sums", tag="bank%d" % (0, 1, 1, 3)[c])
+            sums = psum.tile([P, PACK, CHUNK], F32, name="b_sums", tag="bank%d" % c)
             for t in range(PACK):
                 project(t, wb_q[c], slice(0, CHUNK), sums[:, t, :])
             return sums
@@ -155,6 +159,7 @@ def tile_picked_gramsel_none_p_kernel(tc, x_words, x_scales, wa, wb, gt, gi, off
             nc.vector.tensor_tensor(z_woven[c][:], project_chunk(c)[:].rearrange("p t n -> p n t"), gt_sb[:].unsqueeze(1).to_broadcast([P, CHUNK, PACK]), MULT)
 
         scale_chunk(0)
+        quantise_wb(2)
         scale_chunk(1)
         quantise(nc, *z_q[0], z_woven[0], 0, CHUNK)
         z2_woven = laid("z2_woven", [P, V, PACK], BF16, 1024)

@@ -55,8 +55,8 @@ def tile_picked_gramsel_none_p_kernel(tc, x_words, x_scales, wa, wb, gt, gi, off
         gt_sb = held("gt_sb", [P, PACK], F32)
         gi_sb = held("gi_sb", [P, PACK], F32)
 
-        def load_half(w, h, name):
-            raw = held(name, [P, PACK, HALF], F32)
+        def load_half(w, h, name, offset=None):
+            raw = held(name, [P, PACK, HALF], F32) if offset is None else laid(name, [P, PACK, HALF], F32, offset)
             nc.sync.dma_start(raw[:], w[:, h * HALF : (h + 1) * HALF].rearrange("(p t) c -> p t c", t=PACK))
             return raw
 
@@ -70,7 +70,7 @@ def tile_picked_gramsel_none_p_kernel(tc, x_words, x_scales, wa, wb, gt, gi, off
         nc.sync.dma_start(gi_sb[:], gi.rearrange("(p t) o -> p (t o)", t=PACK))
         nc.sync.dma_start(fa_sb[:], fa)
         wb_raw0 = load_half(wb, 0, "wb_raw0")
-        wb_raw1 = load_half(wb, 1, "wb_raw1")
+        wb_raw1 = load_half(wb, 1, "wb_raw1", 4096)
         nc.sync.dma_start(gt_sb[:], gt.rearrange("(p t) o -> p (t o)", t=PACK))
 
         wa_woven0 = held("wa_woven0", [P, HALF, PACK], BF16)
@@ -146,7 +146,7 @@ def tile_picked_gramsel_none_p_kernel(tc, x_words, x_scales, wa, wb, gt, gi, off
         look_up(2)
         look_up(3)
 
-        z_woven = [held("z_woven0", [P, CHUNK, PACK], BF16, "wb_raw1"), laid("z_woven1", [P, CHUNK, PACK], BF16, 0), held("z_woven2", [P, CHUNK, PACK], BF16, "z2_pairs"), held("z_woven3", [P, CHUNK, PACK], BF16)]
+        z_woven = [laid("z_woven0", [P, CHUNK, PACK], BF16, 4096), laid("z_woven1", [P, CHUNK, PACK], BF16, 5120), held("z_woven2", [P, CHUNK, PACK], BF16, "z2_pairs"), held("z_woven3", [P, CHUNK, PACK], BF16)]
         z_q = [operand("zchunk%d" % c, CHUNK) for c in range(3)]
 
         def project_chunk(c):
@@ -169,7 +169,7 @@ def tile_picked_gramsel_none_p_kernel(tc, x_words, x_scales, wa, wb, gt, gi, off
         quantise(nc, *z2_q, z2_woven, 0, V)
         scale_chunk(2)
         sums = project_chunk(3)
-        z_planes = held("z_planes", [P, PACK, CHUNK], BF16, "a_rows3")
+        z_planes = held("z_planes", [P, PACK, CHUNK], BF16, "a_rows2")
         for t in range(PACK):
             nc.scalar.activation(z_planes[:, t, :], sums[:, t, :], COPY, scale=gt_sb[:, t : t + 1])
         weave(nc.scalar.copy, z_woven[3], z_planes, 0, CHUNK)

@@ -20,7 +20,6 @@ PACK = 4
 HALF = 256
 CHUNK = 128
 WA0_VECTOR = 128
-WA1_SCALAR = 80
 
 
 def weave(copy, dst, src, c0, c1):
@@ -98,9 +97,8 @@ def tile_picked_gramsel_none_p_kernel(tc, x_words, x_scales, wa, wb, gt, gi, off
             multiply(sums, (xq_codes, xq_scales), slice(t * P, (t + 1) * P), weights, cols)
 
         wa_woven1 = held("wa_woven1", [P, HALF, PACK], BF16)
-        weave(nc.scalar.copy, wa_woven1, wa_raw1, 0, WA1_SCALAR)
         weave(nc.vector.tensor_copy, wa_woven1, wa_raw1, CHUNK, HALF)
-        weave(nc.vector.tensor_copy, wa_woven1, wa_raw1, WA1_SCALAR, CHUNK)
+        weave(nc.vector.tensor_copy, wa_woven1, wa_raw1, 0, CHUNK)
         for u in (1, 0):
             quantise(nc, *wa_q[1], wa_woven1, u * CHUNK, (u + 1) * CHUNK)
 
@@ -108,7 +106,7 @@ def tile_picked_gramsel_none_p_kernel(tc, x_words, x_scales, wa, wb, gt, gi, off
         z2_pairs = held("z2_pairs", [P, 2, V, 2], BF16)
 
         def look_up(t):
-            nc.scalar.activation(z2_pairs[:, t // 2, :, t % 2], a_rows[t][:].indirect(fa_sb[:]), COPY)
+            nc.scalar.activation(z2_pairs[:, t // 2, :, t % 2], a_rows[t][:].indirect(fa_sb[:]), COPY, scale=gi_sb[:, t : t + 1])
 
         late = []
         for h, t, bank in ((0, 0, 0), (0, 1, 1), (0, 2, 2), (1, 0, 4), (1, 1, 5), (1, 2, 6), (1, 3, 7), (0, 3, 4)):
@@ -116,9 +114,9 @@ def tile_picked_gramsel_none_p_kernel(tc, x_words, x_scales, wa, wb, gt, gi, off
             project(t, wa_q[h], slice(0, HALF), sums[:])
             dst = a_rows[t][:, h * HALF : (h + 1) * HALF]
             if bank < 6:
-                nc.scalar.activation(dst, sums[:], COPY, scale=gi_sb[:, t : t + 1])
+                nc.scalar.copy(dst, sums[:])
             else:
-                late.append((dst, sums, t))
+                late.append((dst, sums))
             if (h, t) == (1, 1):
                 look_up(0)
                 look_up(1)
@@ -138,8 +136,8 @@ def tile_picked_gramsel_none_p_kernel(tc, x_words, x_scales, wa, wb, gt, gi, off
         weave_wb(0, wb_raw0)
         quantise_wb(0)
         quantise_wb(1)
-        for dst, sums, t in late:
-            nc.vector.tensor_scalar(dst, sums[:], gi_sb[:, t : t + 1], None, MULT)
+        for dst, sums in late:
+            nc.vector.tensor_copy(dst, sums[:])
         weave_wb(1, wb_raw1)
         quantise_wb(3)
 

@@ -113,7 +113,7 @@ def tile_picked_gramsel_none_p_kernel(tc, x_words, x_scales, wa, wb, gt, gi, off
             sums = psum.tile([P, HALF], F32, name="sums", tag="bank%d" % bank)
             project(t, wa_q[h], slice(0, HALF), sums[:])
             dst = a_rows[t][:, h * HALF : (h + 1) * HALF]
-            if bank < 6:
+            if bank < 6 and t < 3:
                 nc.scalar.copy(dst, sums[:])
             else:
                 late.append((dst, sums))
@@ -122,7 +122,7 @@ def tile_picked_gramsel_none_p_kernel(tc, x_words, x_scales, wa, wb, gt, gi, off
                 look_up(1)
 
         wb_woven1 = laid("wb_woven1", [P, HALF, PACK], BF16, 0)
-        wb_woven = [a_rows[2 + u][:, HALF:H].bitcast(BF16).rearrange("p (c t) -> p c t", t=PACK) for u in range(2)]
+        wb_woven = [scratch.bitcast(BF16).rearrange("p (c t) -> p c t", t=PACK) for scratch in (a_rows[2][:, HALF:H], a_rows[3][:, CHUNK : CHUNK + HALF])]
         wb_woven.extend(wb_woven1[:, u * CHUNK : (u + 1) * CHUNK, :] for u in range(2))
         wb_q = [operand("wb%d" % c, CHUNK) for c in range(H // CHUNK)]
 
@@ -159,9 +159,9 @@ def tile_picked_gramsel_none_p_kernel(tc, x_words, x_scales, wa, wb, gt, gi, off
         scale_chunk(0)
         quantise_wb(2)
         scale_chunk(1)
-        quantise(nc, *z_q[0], z_woven[0], 0, CHUNK)
         z2_woven = laid("z2_woven", [P, V, PACK], BF16, 1024)
         nc.vector.tensor_copy(z2_woven[:].bitcast(I32), z2_pairs[:].rearrange("p u v e -> p u (v e)").bitcast(I32).rearrange("p u v -> p v u"))
+        quantise(nc, *z_q[0], z_woven[0], 0, CHUNK)
         quantise(nc, *z_q[1], z_woven[1], 0, CHUNK)
         z2_q = operand("z2", V)
         quantise(nc, *z2_q, z2_woven, 0, V)

@@ -136,9 +136,10 @@ def tile_picked_gramsel_none_p_kernel(tc, x_words, x_scales, wa, wb, gt, gi, off
         weave_wb(0, wb_raw0)
         quantise_wb(0)
         quantise_wb(1)
-        for dst, sums in late:
+        for dst, sums in late[:2]:
             nc.vector.tensor_copy(dst, sums[:])
         weave_wb(1, wb_raw1)
+        nc.vector.tensor_copy(late[2][0], late[2][1][:])
         quantise_wb(3)
 
         look_up(2)

from contextlib import ExitStack

import concourse.mybir as mybir

K, T, S, V, H = 512, 2048, 512, 256, 512
FLOPS = 2 * K * S * H * 2 + 2 * S * H * V

F32 = mybir.dt.float32
BF16 = mybir.dt.bfloat16
I32 = mybir.dt.int32
U32 = mybir.dt.uint32
U16 = mybir.dt.uint16
U8 = mybir.dt.uint8
FP8X4 = mybir.dt.float8_e4m3fn_x4
COPY = mybir.ActivationFunctionType.Copy
MULT = mybir.AluOpType.mult

P = 128
PACK = 4
HALF = 256
CHUNK = 128
WA0_VECTOR = 128


def weave(copy, dst, src, c0, c1):
    copy(dst[:, c0:c1, :].rearrange("p (c i) t -> p c t i", i=4), src[:, :, c0:c1].rearrange("p t (c i) -> p c t i", i=4))


def quantise(nc, codes, scales, woven, c0, c1):
    nc.vector.quantize_mx(out=codes[:, c0:c1].bitcast(FP8X4), scales=scales[:, c0:c1], in_=woven[:, c0:c1, :].rearrange("p c t -> p (c t)"))


def tile_picked_gramsel_none_p_kernel(tc, x_words, x_scales, wa, wb, gt, gi, offs, fa, out):
    nc = tc.nc
    with ExitStack() as ctx:
        lists = ctx.enter_context(tc.tile_pool(name="lists", bufs=1))
        keep = ctx.enter_context(tc.tile_pool(name="keep", bufs=1))
        shared = ctx.enter_context(tc.tile_pool(name="shared", bufs=1))
        psum = ctx.enter_context(tc.psum_pool(name="psum", bufs=1))

        def held(name, shape, dtype, tag=None):
            return keep.tile(shape, dtype, name=name, tag=tag or name, align_bytes=64)

        def laid(name, shape, dtype, offset):
            return shared.tile(shape, dtype, name=name, offset=offset, align_bytes=64)

        def operand(name, width, codes_tag=None, scales_tag=None):
            return held(name + "_codes", [P, width], U32, codes_tag), held(name + "_scales", [P, width], U8, scales_tag)

        offs_sb = lists.tile([P, S // 16], U16, name="offs_sb")
        fa_sb = lists.tile([P, V // 16], U16, name="fa_sb")
        xw = held("xw", [P, T], U32)
        xs = held("xs", [P, T], U8)
        gt_sb = held("gt_sb", [P, PACK], F32)
        gi_sb = held("gi_sb", [P, PACK], F32)

        def load_half(w, h, name, offset=None):
            raw = held(name, [P, PACK, HALF], F32) if offset is None else laid(name, [P, PACK, HALF], F32, offset)
            nc.sync.dma_start(raw[:], w[:, h * HALF : (h + 1) * HALF].rearrange("(p t) c -> p t c", t=PACK))
            return raw

        nc.vector.memset(xs[:].bitcast(I32), 0)
        wa_raw0 = load_half(wa, 0, "wa_raw0")
        nc.sync.dma_start(offs_sb[:], offs)
        for q in range(4):
            nc.sync.dma_start(xs[32 * q : 32 * q + 4, :].bitcast(I32), x_scales[0, 4 * q : 4 * q + 4, :].bitcast(I32))
        nc.sync.dma_start(xw[:].bitcast(I32), x_words[0].rearrange("p n t -> p (n t)").bitcast(I32))
        wa_raw1 = load_half(wa, 1, "wa_raw1")
        nc.sync.dma_start(gi_sb[:], gi.rearrange("(p t) o -> p (t o)", t=PACK))
        nc.sync.dma_start(fa_sb[:], fa)
        wb_raw0 = load_half(wb, 0, "wb_raw0")
        wb_raw1 = load_half(wb, 1, "wb_raw1", 4096)
        nc.sync.dma_start(gt_sb[:], gt.rearrange("(p t) o -> p (t o)", t=PACK))

        wa_woven0 = held("wa_woven0", [P, HALF, PACK], BF16)
        weave(nc.vector.tensor_copy, wa_woven0, wa_raw0, 0, WA0_VECTOR)
        weave(nc.scalar.copy, wa_woven0, wa_raw0, WA0_VECTOR, HALF)
        wa_q = [operand("wa0", HALF), operand("wa1", HALF)]
        quantise(nc, *wa_q[0], wa_woven0, 0, HALF)
        xq_scales = held("xq_scales", [P, S], U8, "wa_woven0")
        nc.vector.tensor_copy(xq_scales[:].rearrange("p (t m) -> p m t", t=PACK), xs[:].indirect(offs_sb[:]))
        xq_codes = held("xq_codes", [P, S], U32)
        nc.vector.tensor_copy(xq_codes[:].rearrange("p (t m) -> p m t", t=PACK), xw[:].indirect(offs_sb[:]))

        def multiply(sums, stationary, rows, moving, cols):
            nc.tensor.matmul_mx(
                out=sums,
                lhsT=stationary[0][:, rows].bitcast(FP8X4),
                lhsT_scale=stationary[1][:, rows],
                rhs=moving[0][:, cols].bitcast(FP8X4),
                rhs_scale=moving[1][:, cols],
                start=True,
                stop=True,
            )

        def project(t, weights, cols, sums):
            multiply(sums, (xq_codes, xq_scales), slice(t * P, (t + 1) * P), weights, cols)

        wa_woven1 = held("wa_woven1", [P, HALF, PACK], BF16)
        weave(nc.vector.tensor_copy, wa_woven1, wa_raw1, CHUNK, HALF)
        weave(nc.vector.tensor_copy, wa_woven1, wa_raw1, 0, CHUNK)
        for u in (1, 0):
            quantise(nc, *wa_q[1], wa_woven1, u * CHUNK, (u + 1) * CHUNK)

        a_rows = [held("a_rows%d" % t, [P, H], F32) for t in range(PACK)]
        z2_pairs = held("z2_pairs", [P, 2, V, 2], BF16)

        def look_up(t):
            nc.scalar.activation(z2_pairs[:, t // 2, :, t % 2], a_rows[t][:].indirect(fa_sb[:]), COPY, scale=gi_sb[:, t : t + 1])

        late = []
        for h, t, bank in ((0, 0, 0), (0, 1, 1), (0, 2, 2), (1, 0, 4), (1, 1, 5), (1, 2, 6), (1, 3, 7), (0, 3, 4)):
            sums = psum.tile([P, HALF], F32, name="sums", tag="bank%d" % bank)
            project(t, wa_q[h], slice(0, HALF), sums[:])
            dst = a_rows[t][:, h * HALF : (h + 1) * HALF]
            if bank < 6 and t < 3:
                nc.scalar.copy(dst, sums[:])
            else:
                late.append((dst, sums))
            if (h, t) == (1, 1):
                look_up(0)
                look_up(1)

        wb_woven1 = laid("wb_woven1", [P, HALF, PACK], BF16, 0)
        wb_woven = [scratch.bitcast(BF16).rearrange("p (c t) -> p c t", t=PACK) for scratch in (a_rows[2][:, HALF:H], a_rows[3][:, CHUNK : CHUNK + HALF])]
        wb_woven.extend(wb_woven1[:, u * CHUNK : (u + 1) * CHUNK, :] for u in range(2))
        wb_q = [operand("wb%d" % c, CHUNK) for c in range(H // CHUNK)]

        def weave_wb(h, raw):
            for u in (h, 1 - h):
                weave(nc.vector.tensor_copy, wb_woven[2 * h + u], raw[:, :, u * CHUNK : (u + 1) * CHUNK], 0, CHUNK)

        def quantise_wb(c):
            quantise(nc, *wb_q[c], wb_woven[c], 0, CHUNK)

        weave_wb(0, wb_raw0)
        quantise_wb(0)
        quantise_wb(1)
        for dst, sums in late[:2]:
            nc.vector.tensor_copy(dst, sums[:])
        weave_wb(1, wb_raw1)
        nc.vector.tensor_copy(late[2][0], late[2][1][:])
        quantise_wb(3)

        look_up(2)
        look_up(3)

        z_woven = [laid("z_woven0", [P, CHUNK, PACK], BF16, 4096), laid("z_woven1", [P, CHUNK, PACK], BF16, 5120), held("z_woven2", [P, CHUNK, PACK], BF16, "z2_pairs"), held("z_woven3", [P, CHUNK, PACK], BF16)]
        z_q = [operand("zchunk%d" % c, CHUNK) for c in range(3)]

        def project_chunk(c):
            sums = psum.tile([P, PACK, CHUNK], F32, name="b_sums", tag="bank%d" % c)
            for t in range(PACK):
                project(t, wb_q[c], slice(0, CHUNK), sums[:, t, :])
            return sums

        def scale_chunk(c):
            nc.vector.tensor_tensor(z_woven[c][:], project_chunk(c)[:].rearrange("p t n -> p n t"), gt_sb[:].unsqueeze(1).to_broadcast([P, CHUNK, PACK]), MULT)

        scale_chunk(0)
        quantise_wb(2)
        scale_chunk(1)
        z2_woven = laid("z2_woven", [P, V, PACK], BF16, 1024)
        nc.vector.tensor_copy(z2_woven[:].bitcast(I32), z2_pairs[:].rearrange("p u v e -> p u (v e)").bitcast(I32).rearrange("p u v -> p v u"))
        quantise(nc, *z_q[0], z_woven[0], 0, CHUNK)
        quantise(nc, *z_q[1], z_woven[1], 0, CHUNK)
        z2_q = operand("z2", V)
        quantise(nc, *z2_q, z2_woven, 0, V)
        scale_chunk(2)
        sums = project_chunk(3)
        z_planes = held("z_planes", [P, PACK, CHUNK], BF16, "a_rows2")
        for t in range(PACK):
            nc.scalar.activation(z_planes[:, t, :], sums[:, t, :], COPY, scale=gt_sb[:, t : t + 1])
        weave(nc.scalar.copy, z_woven[3], z_planes, 0, CHUNK)
        z_q.append((held("zchunk3_codes", [P, CHUNK], U32), laid("zchunk3_scales", [P, CHUNK], U8, 2048)))
        for c in (3, 2):
            quantise(nc, *z_q[c], z_woven[c], 0, CHUNK)

        def product(c, cols, bank):
            sums = psum.tile([P, cols.stop - cols.start], F32, name="out_sums", tag="bank%d" % bank)
            multiply(sums[:], z_q[c], slice(0, CHUNK), z2_q, cols)
            return sums

        def on_vector(dst, sums):
            nc.vector.tensor_scalar(dst, sums[:], 0.0625, None, MULT)

        def on_scalar(dst, sums):
            nc.scalar.activation(dst, sums[:], COPY, scale=0.0625)

        for c, banks in ((0, (4,)), (1, (5,)), (3, (6, 7)), (2, (0, 1))):
            result = held("result%d" % c, [P, V], F32)
            if len(banks) == 2:
                for cols, bank, empty in ((slice(0, V // 2), banks[0], on_vector), (slice(V // 2, V), banks[1], on_scalar)):
                    empty(result[:, cols], product(c, cols, bank))
                    if c == 2:
                        nc.sync.dma_start(out[c * CHUNK : (c + 1) * CHUNK, cols], result[:, cols])
            else:
                on_scalar(result[:], product(c, slice(0, V), banks[0]))
            if c != 2:
                nc.sync.dma_start(out[c * CHUNK : (c + 1) * CHUNK, :], result[:])
